import numpy as np, ml_dtypes
CORES = [40,41,42,43,44,45,46,47]
N = 8
BF = ml_dtypes.bfloat16
def gentries(a):
    return np.ascontiguousarray(a.reshape(8, 16, -1).transpose(0, 2, 1)).reshape(8, -1)
def gtable(e):
    e = np.asarray(e); return np.ascontiguousarray(e.reshape(8, -1, 16).transpose(0, 2, 1)).reshape(128, -1).astype(np.int32)
V, H, B, RO, GM, LG = 512, 3, 4, 3, 2047, 11
def parts(rng):
    s = (N, 8, 16, V)
    return (rng.integers(0, 256, s), rng.integers(1, GM + 1, s), (rng.random(s) < rng.choice(np.array([0.25, 0.4, 0.55]), (N, 8, 1, 1))).astype(np.int64),
            rng.integers(0, V, (N, 8, V)), rng.integers(50, 63, s))
def pack(c, g, p, f, t):
    def flat(a): return np.ascontiguousarray(a.reshape(N, 128, V)).astype(np.int32)
    return {"c0": flat(c).astype(np.float32).astype(BF), "gp": flat(g), "cp": flat(p), "rf": np.stack([gtable(a) for a in f]), "th": flat(t)}
def setup_inputs(rng):
    return pack(*parts(rng))
def setup_inputs_spread(rng):
    c, g, p, f, t = parts(rng)
    c = np.minimum((np.exp2(8 * rng.random((N, 1, 1, V))) * rng.random(c.shape)).astype(np.int64), 255)
    g = np.minimum(np.maximum(np.exp2(LG * rng.random(g.shape)).astype(np.int64), 1), GM)
    p = (rng.random(p.shape) < rng.random((N, 8, 1, V))).astype(np.int64)
    f = np.minimum((V * rng.random(f.shape) ** 3).astype(np.int64), V - 1)
    return pack(c, g, p, f, rng.integers(0, 129, t.shape))
def setup_inputs_ends(rng):
    s = (N, 8, 16, V)
    def runs(v): return np.repeat(rng.choice(np.array(v), (N, 1, 1, V // 32)), 32, axis=3)
    c = np.where(np.where(runs([0, 1]) == 1, rng.random(s), rng.random((N, 1, 1, V))) < runs([0.1, 0.5, 0.9]), 255, 0)
    c[..., :17] = 255; c[..., V - 17:V - 1] = 255; c[..., V - 1] = 0; c[..., 64:128] = 0
    g = np.where(rng.random(s) < rng.choice(np.array([0.0, 0.5, 1.0]), (N, 8, 1, V)), GM, 1)
    p = (rng.random(s) < rng.choice(np.array([0.0, 0.0, 0.5, 0.8, 1.0]), (N, 8, 1, V))).astype(np.int64)
    p[:, :, 0, V - 1] = 0; p[N - 1, 7, :, V - 1] = 0; g[N - 1, 7, :, V - 1] = GM; p[:, :, :, 96] = 0
    f = (V - 1) * rng.integers(0, 2, (N, 8, V))
    t = 128 * np.where(rng.random((N, 8, 1, V)) < 0.5, rng.integers(0, 2, (N, 8, 1, V)), rng.integers(0, 2, s)); t[:, :, 0, V - 1] = 128
    return pack(c, g, p, f, t)
def setup_inputs_corners(rng):
    c, g, p, f, t = parts(rng); v = np.arange(V); k = np.arange(16)
    kinds = [v * 0, v * 0 + V - 1, v, np.maximum(v - 1, 0), np.minimum(v + 1, V - 1), v ^ 1, V - 1 - v]
    o = np.argsort(rng.random((N, 8)), axis=1)
    for q in range(N):
        for a in range(8): f[q, o[q, a]] = kinds[a] if a < 7 else rng.choice(np.array([0, V - 1]), V)
    one = rng.integers(0, 8, (N, 8, V)); run = np.repeat(rng.integers(0, 8, (N, 8, V // 16)), 16, axis=2)
    w = np.where(np.repeat(rng.random((N, 8, V // 16)) < 0.5, 16, axis=2), run, one)
    pat = np.stack([k < 0, k >= 0, k == 0, k == 15, k != 0, k != 15, (k & 1) == 1]).astype(np.int64)
    p = np.where(w[:, :, None, :] == 7, p, pat[np.minimum(w, 6)].transpose(0, 1, 3, 2))
    g = np.where(rng.random((N, 8, 1, V)) < 0.3, rng.choice(np.array([1, GM]), (N, 8, 1, V)), g)
    u = rng.random((N, 1, 1, V)); u[0, :, :, 0] = 0.5; u[N // 2 - 1::N // 2, :, :, V - 24:] = 0.5
    c = np.where(u < 0.1, 0, np.where(u > 0.9, 255, c)); t = rng.choice(np.array([0, 1, 52, 56, 60, 127, 128]), t.shape)
    for q in range(N - 1):
        a, b, e = o[q, 0], o[q, 1], o[q, 3]; i, j = rng.permutation(16)[:2]
        p[q, a] = 1; p[q, b] = 0; p[q, e, i] = 1; p[q, e, j] = 0
        g[q, b] = rng.integers(1, 4, (16, V)); g[q, b, 0] = V - v + rng.integers(0, V - 64, V)
    p[N - 1, :, :, V - 1] = 0; g[N - 1, :, :, V - 1] = GM; t[N - 1, :, :, V - 1] = 128
    return pack(c, g, p, f, t)
def setup_inputs_crowd(rng):
    c, g, p, f, t = parts(rng); s = c.shape
    u = rng.random((N, 1, 1, V)); u[..., 0] = 0.0; u[..., V - 1] = 0.0; u[..., 1] = 0.9; u[..., V - 2] = 0.9
    low = u < 0.03125; mixed = (u >= 0.03125) & (u < 0.15625)
    miss = (rng.random((N, 8, 1, V)) < 0.1) & (np.arange(16)[:, None] == rng.integers(0, 16, (N, 8, 1, V)))
    z = np.where(low, 0, np.where(mixed, rng.integers(0, 2, s), np.where(miss, 0, 1)))
    c = 2 * rng.integers(0, 128, (1, 8, 16, 1)) + z
    t = np.where(low, rng.integers(127, 129, s), np.where(mixed, rng.integers(48, 63, s), rng.integers(0, 5, s)))
    for q in range(N):
        a = rng.integers(0, 8); x = rng.integers(0, V); f[q, a] = x; p[q, a] = 1; p[q, a, :, x] = 0; p[q, a, :, V - 1] = 0
    return pack(c, g, p, f, t)
def check_inputs(d):
    bad = []
    for k, lo, hi in (("c0", 0, 255), ("gp", 1, GM), ("cp", 0, 1), ("rf", 0, V - 1), ("th", 0, 128)):
        a = np.asarray(d[k]).astype(np.float64)
        if not (np.min(a) >= lo and np.max(a) <= hi): bad.append("range of " + k)
        elif np.any(a != np.floor(a)): bad.append("whole numbers in " + k)
    return bad
def reference(c0, gp, cp, rf, th):
    C = c0.astype(np.float32).astype(np.int32).reshape(N, 8, 16, V); g = gp.astype(np.int64).reshape(N, 8, 16, V)
    own = cp.reshape(N, 8, 16, V) == 0; t = th.astype(np.int64).reshape(N, 8, 16, V)
    rl = np.stack([gentries(a) for a in rf]).astype(np.int64)[:, :, None, :]; base = np.arange(N * V).reshape(N, 1, 1, V)
    for rnd in range(RO):
        G = (base + np.add.accumulate(np.where(own, g, 0), axis=2)) & (N * V - 1)
        S = G
        for h in range(H): S = np.where(own, G, np.take_along_axis(S, rl, 3))
        T = np.ascontiguousarray(C.transpose(1, 2, 0, 3)).reshape(8, 16, N * V)
        f = []; new = []
        for r in range(N):
            P = np.take_along_axis(T, S[r].reshape(8, 1, 16 * V), 2).reshape(8, 16, 16, V)
            f.append(np.add.reduce((P > C[r][:, :, None, :]).astype(np.int64), axis=(0, 1)))
            best = np.maximum.reduce(P.reshape(8, 16, B, 16 // B, V), axis=3)
            new.append((C[r] + np.add.reduce(best, axis=2)) & 255)
        m = own & (np.stack(f)[:, None] < t)
        first = m & (np.add.accumulate(m.astype(np.int64), axis=2) == 1)
        g = g + first.astype(np.int64); C = np.stack(new)
    return {"yc": C.reshape(N, 128, V).astype(np.float32).astype(BF), "yg": g.reshape(N, 128, V).astype(np.float32)}

@@ -1,0 +1,460 @@
+from concourse.bass import DstId, RemoteDMATransfer
+from concourse.mybir import AluOpType as ALU, AxisListType, ActivationFunctionType as ACT
+
+V = 512
+CH = 128
+TW = 4096 + 16
+HUGE = 1048576.0
+ROUND = 12582912.0
+BIG = 40960.0
+
+SCRATCH = {
+    "T0": ("sbuf", [128, TW], "bfloat16"), "T1": ("sbuf", [128, TW], "bfloat16"), "T2": ("sbuf", [128, TW], "bfloat16"),
+    "cout": ("sbuf", [128, V], "bfloat16"), "gout": ("sbuf", [128, V], "float32"),
+    "gpi": ("sbuf", [128, V], "int32"), "cpi": ("sbuf", [128, V], "int32"), "thi": ("sbuf", [128, V], "int32"),
+    "rfi": ("sbuf", [128, 32], "int32"),
+    "P": ("sbuf", [128, 16 * V], "bfloat16"), "M": ("sbuf", [128, 16 * V], "bfloat16"), "B": ("sbuf", [128, 16 * V], "bfloat16"),
+    "RM": ("sbuf", [128, 16 * CH], "bfloat16"),
+    "J": ("sbuf", [128, 144], "float32"), "K": ("sbuf", [128, 128], "float32"), "pos2": ("sbuf", [128, V], "float32"),
+    "eye": ("sbuf", [128, 128], "bfloat16"), "neye": ("sbuf", [128, 128], "bfloat16"), "heye": ("sbuf", [128, 128], "bfloat16"),
+    "eye16": ("sbuf", [128, 128], "float16"), "zs": ("sbuf", [128, 128], "bfloat16"), "jge": ("sbuf", [128, 128], "bfloat16"),
+    "tri": ("sbuf", [128, 128], "bfloat16"), "tri16": ("sbuf", [128, 128], "float16"), "bd": ("sbuf", [128, 128], "bfloat16"),
+    "j1": ("sbuf", [128, 128], "bfloat16"), "k0": ("sbuf", [128, 128], "float32"), "pm0": ("sbuf", [128, 8], "float32"),
+    "wsel": ("sbuf", [128, 144], "float32"), "en": ("sbuf", [128, 144], "bfloat16"),
+    "half": ("sbuf", [128, 128], "float32"), "c192": ("sbuf", [128, 128], "bfloat16"), "c256": ("sbuf", [128, 256], "bfloat16"),
+    "zero": ("sbuf", [128, 128], "bfloat16"),
+    "l1": ("sbuf", [128, 32], "uint16"), "l1a": ("sbuf", [128, 32], "uint16"), "l23": ("sbuf", [128, 64], "uint16"),
+    "r1": ("sbuf", [128, V], "float32"), "r23": ("sbuf", [128, 2 * V], "float32"),
+    "ownb": ("sbuf", [128, V], "bfloat16"), "cpb": ("sbuf", [128, V], "bfloat16"), "thb": ("sbuf", [128, V], "bfloat16"),
+    "og": ("sbuf", [128, V], "float16"), "cp1": ("sbuf", [128, V], "bfloat16"), "cp2": ("sbuf", [128, V], "bfloat16"),
+    "kst": ("sbuf", [128, V], "bfloat16"), "eyeh": ("sbuf", [128, 128], "bfloat16"),
+    "x0": ("sbuf", [128, V], "float32"), "x1": ("sbuf", [128, V], "float32"), "x2": ("sbuf", [128, V], "float32"),
+    "x3": ("sbuf", [128, V], "int32"),
+    "u1": ("sbuf", [128, V], "float32"), "u2": ("sbuf", [128, V], "float32"), "u3": ("sbuf", [128, V], "float32"),
+    "soff": ("sbuf", [128, V], "uint16"), "s16": ("sbuf", [128, V], "float16"),
+    "yq": ("sbuf", [128, V], "bfloat16"), "mb": ("sbuf", [128, V], "bfloat16"),
+    "W0": ("sbuf", [128, 2 * V], "bfloat16"), "W1": ("sbuf", [128, 2 * V], "bfloat16"), "W2": ("sbuf", [128, V], "bfloat16"),
+    "t1": ("sbuf", [128, V], "bfloat16"), "t2": ("sbuf", [128, V], "bfloat16"), "t3": ("sbuf", [128, V], "bfloat16"),
+    "CR0": ("psum", [128, 512], "float32"), "CR1": ("psum", [128, 512], "float32"), "X": ("psum", [128, 512], "float32"),
+    "F0": ("psum", [128, 512], "float32"), "F1": ("psum", [128, 512], "float32"), "CM": ("psum", [128, 512], "float32"),
+    "D0": ("psum", [128, 512], "float32"), "D1": ("psum", [128, 512], "float32"),
+}
+PSUM = [k for k in SCRATCH if SCRATCH[k][0] == "psum"]
+SEMAPHORES = ["qv", "qs", "qp", "qg", "ldc", "ldg", "ldp", "ldr", "ldt", "arr0", "arr1a", "arr1b", "arr1c", "arr2a", "arr2b", "arr2c",
+              "sent0", "sent", "st"]
+COUNTER = {"v": "qv", "s": "qs", "p": "qp", "g": "qg"}
+OPT = {"r0": 128,
+       "shifts": [(0, 128, "vsv"), (128, 256, "svs"), (256, 512, "vss")],
+       "rounds": [{"cuts": [0, 128, 256, 384, 512], "gathers": [0, 64, 128, 256, 384, 512], "by_v": [64], "high_v": ["a", "a", ""][r],
+                   "scans": [0, 128, 256, 384, 512],
+                   "sends": [[256, 512], [256, 512], [384, 512]][r], "order": [0, 1, 2, 3], "by_s": [0, 0, 0, [2, 2, 3][r]],
+                   "banks": ["D0", "D1"], "fbank": ["F0", "F0", "F1", "F0"], "gaps": [0, 384, 512],
+                   "boost": [6000.0, 6000.0, 0.0][r]} for r in range(3)],
+       "g": 1.3, "e": 1.04, "pe": 0.53, "hop": 80.0}
+PLAN = {}
+
+
+ORDER = (
+    "00040b010d02030c060j1r0k0h0f0g0i0e0l050y1d0n0o0p070s0x0m0a0A2r2s2t0q2u210t220z23240u1s0C0B0D0E290r0F0v0G0H1g0I0J0M3r0K3s3t3u3v1e0N3y3z3A3B3C0L1h0O0R1f0U0P080V090S0W0X0Y0Q0Z0T101k11121l131415161i171m18191q251t1u1v1w1y1z262a2b2c2d1n272e2f2g2h1x2i2j2k2l281A1B1C1D1c2W2m2n2X2Y1j2o1E2p2q2z2Z2v2A1o34351F2B2C2D1I2E1G1J1K2w1L1M1N1O1Q1R2x2F2G2H2I2y2J2K2L2M1P2N2O2P2Q3D2R3w3E3F3L301S1T1U1V3G1W3M1b361H1a373x2S1X3839313H1Y3I3N3O3P3Q323a203b3c3d2T333e3f3g2U3R2V3J3h3S3T3U3i3j3k3K3n3l3V3m3W3X3Y1p3o3p3Z3q400w41424843444945464a474i4j4s4t4d4f4u1Z4b4l4k4J5r4n4z4c4e4v4g4m4p4o5s5J4h4x4w4q4D5K4C4y4A5L5M6m4K6Q6R6S6T4r6n6U4B4E6J4I5j5k5l5m6K6L6M6N6a5n4L4M4N4O4Q4R5o5t5u5v5w5p5x5y4F5z5A4P5B5C5D5E5q4S4T4U4V4W5F5G5H5N5I5R6e6f4G5S6g6h4X5T5U5V505W4Y51525O5354555658595P5X5Y5Z605Q6162636457656667686O696X6Y6P6Z73706i5a5b5c5d6V5e4H4Z6o6p6W6q5f6r6b6j6c5g746d757677786k6s5i6t6u6v6F796l6w6x6y6z7a7b716A6B6C6D7c6E7q727d6G6H7e6I7f7g7h7i7j7k7m7l7r7s7n7o7A7p7B7C7K7L7t7v7M7x7D7u5h7w7H7N7y7E7P809y7z7O7F7R7Q7V7G7I7U7S8F9z8Ga08Xa1a2a3a47J818Y7T8Z7W907Z8x8y8z8A9T9U9V9W9X8B8283848587888D8H8I8J8K8C7X8E8L8M8N8O8P8Q929q9r9s9t8R8S918T8U8V8W9596949798999a9b9c937Y9d9e86adaeafag9f9g9h9i9j9k9l9m9u898a8b8c8e8f8d9A9B9C9D9na59oa6aiaj9v9Y8g9Z8h8i9w9E9F9G9HaD9p9x9I9J9K8j9L8kak8n9Ma79N9O9Pa89Qa9aaabaEahac9Ralamanao8l9SapaqarasaF8mataGauavawaxayazaH8oaA8p8q8r8s8taB8uaIaJaC8vaK8waLaM"
+)
+
+
+def arrange(tasks):
+    d = "0123456789abcdefghijklmnopqrstuvwxyzABCDEFGHIJKLMNOPQRSTUVWXYZ"
+    seq = [62 * d.index(ORDER[i]) + d.index(ORDER[i + 1]) for i in range(0, len(ORDER), 2)]
+    assert sorted(seq) == list(range(len(tasks)))
+    return seq
+
+
+def rank_program(g, core, T, topo):
+    rank = T.rank_of(core)
+    if rank is None:
+        return
+    n_ranks = len(T.cores)
+    own = V * rank
+    queue = {"v": g.vector, "s": g.scalar, "p": g.tensor, "g": g, "y": g.sync}
+    tasks = []
+    touches = {}
+
+    def A(name, lo, hi, step=1, parts=None):
+        t = T[name]
+        if parts is not None:
+            ap = t[0:parts, lo:hi]
+        elif step > 1:
+            ap = t[:, lo:hi:step]
+        else:
+            ap = t[:, lo:hi]
+        return ap, (name, lo, hi, len(range(lo, hi, step)))
+
+    def task(q, call, reads, writes, cost, sem=None, count=0, lat=0.0, dma=0.0, also=()):
+        deps = set(also)
+        for rs, w in ((reads, False), (writes, True)):
+            for r in rs:
+                for lo2, hi2, w2, q2, j in touches.get(r[0], []):
+                    if (q2 != q or q == "p") if r[0] in PSUM else ((w or w2) and r[1] < hi2 and lo2 < r[2]):
+                        deps.add(j)
+        for rs, w in ((reads, False), (writes, True)):
+            for r in rs:
+                old = touches.get(r[0], [])
+                if r[0] in PSUM:
+                    old = [] if q == "p" else old
+                elif w and len(r) > 3 and r[3] == r[2] - r[1]:
+                    old = [x for x in old if not (r[1] <= x[0] and x[1] <= r[2])]
+                touches[r[0]] = old + [(r[1], r[2], w, q, len(tasks))]
+        kind = "g" if any(SCRATCH[r[0]][2] == "uint16" for r in reads) and writes[0][0] != "s16" else "p" if q == "p" else "e" if q in "vs" and not dma else "o"
+        tasks.append({"q": q, "call": call, "deps": sorted(deps), "cost": cost, "sem": sem, "count": count, "lat": lat, "dma": dma,
+                      "kind": kind})
+        return len(tasks) - 1
+
+    def ind(win, off):
+        return win[0].indirect(off[0]), win[1], off[1]
+
+    def regs(*xs):
+        return [r for x in xs if isinstance(x, tuple) for r in x[1:]]
+
+    def val(x):
+        return x[0] if isinstance(x, tuple) else x
+
+    def narrow(*xs):
+        return 0.5 if all(SCRATCH[x[1][0]][2] in ("bfloat16", "float16", "uint16") for x in xs) else 1.0
+
+    def price(out, a, k):
+        n = out[1][3]
+        return 60.0 + n * OPT["g"] if len(a) == 3 else 50.0 + max(64.0, n * k) * OPT["e"]
+
+    def ts(out, a, s1, s2, op0, op1=None):
+        if op1 is None:
+            call = lambda: g.vector.tensor_scalar(out[0], a[0], val(s1), None, op0)
+        else:
+            call = lambda: g.vector.tensor_scalar(out[0], a[0], val(s1), val(s2), op0, op1)
+        task("v", call, regs(a, s1, s2), regs(out), price(out, a, narrow(out, a)))
+
+    def tt(out, a, b, o):
+        k = 1.0 if a[1][0] in PSUM or b[1][0] in PSUM else 2.0
+        task("v", lambda: g.vector.tensor_tensor(out[0], a[0], b[0], o), regs(a, b), regs(out), price(out, a, k))
+
+    def cp(out, a):
+        task("v", lambda: g.vector.tensor_copy(out[0], a[0]), regs(a), regs(out), price(out, a, narrow(out, a)))
+
+    def fill(out, c):
+        task("v", lambda: g.vector.memset(out[0], c), [], regs(out), price(out, out, narrow(out)))
+
+    def act(out, a, func, bias=0.0, scale=1.0, more=0.0):
+        task("s", lambda: g.scalar.activation(out[0], a[0], func, bias=bias, scale=scale), regs(a), regs(out), more + price(out, a, 1.0))
+
+    def step(out, a):
+        act(out, a, ACT.Sigmoid, bias=-128.0, scale=256.0)
+
+    def mm(out, lhs, rhs, start, stop):
+        k = 4.0 if SCRATCH[rhs[1][0]][2] == "float32" else 1.0
+        task("p", lambda: g.tensor.matmul(out[0], lhs[0], rhs[0], start, stop), regs(lhs, rhs), regs(out),
+             20.0 + max(64, out[1][3]) * k * OPT["pe"])
+
+    def iota(out, pattern, base, mult):
+        task("g", lambda: g.iota(out[0], pattern, base, mult, allow_small_or_imprecise_dtypes=True), [], regs(out),
+             130.0 + 2 * out[1][3] * OPT["e"])
+
+    def load(q, out, src, sem, busy, also=()):
+        return task(q, lambda: queue[q].dma_start(out[0], src), [], regs(out), 100.0, sem, 16, 1700.0 + busy, busy, also)
+
+    def store(dst, a, busy):
+        task("y", lambda: g.sync.dma_start(dst, a[0]), regs(a), [], 100.0, "st", 16, 1700.0 + busy, busy)
+
+    others = [T.cores[(rank + d) % n_ranks] for d in range(1, n_ranks)]
+    mask = topo.mask(core, others[0])
+    for o in others:
+        mask &= topo.mask(core, o)
+    n_eng = bin(mask).count("1")
+    ids = [DstId(rid=topo.addr(o)[0], pnc=topo.addr(o)[1]) for o in others]
+
+    def share(table, lo, hi, arr, loc, more=0.0):
+        src = A(table, own + lo, own + hi)
+        busy = 56 * (35.0 + (hi - lo) / 10.0)
+
+        def call():
+            g.remote_dma_fused([RemoteDMATransfer(dst_ids=ids, dma_engine_mask=mask, remote_sem=T.sem[arr], srcs=[src[0]],
+                                                  dsts=[src[0] for o in others])], local_sem=T.sem[loc])
+        i = task("g", call, regs(src), [], 600.0, loc, n_eng, 1200.0 + more + busy, busy)
+        landed = [(table, V * r + lo, V * r + hi) for r in range(n_ranks) if r != rank]
+        task("far", None, [], landed, 200.0, arr, n_eng * (n_ranks - 1), also=[i])
+        return i
+
+    EYE, NEYE, HEYE, EYE16 = A("eye", 0, 128), A("neye", 0, 128), A("heye", 0, 128), A("eye16", 0, 128)
+    TRI, BD = A("tri", 0, 128), A("bd", 0, 128)
+    L1 = A("l1", 0, 32)
+
+    def full(name):
+        return A(name, 0, V)
+
+    i = load("y", A("T0", own, own + V), T.c0[:], "ldc", 700.0)
+    for out, src, sem, busy in ((A("rfi", 0, 32), T.rf[:], "ldr", 330.0), (full("cpi"), T.cp[:], "ldp", 1100.0),
+                                (full("gpi"), T.gp[:], "ldg", 1100.0)):
+        j = load("y", out, src, sem, busy)
+        tasks[j]["behind"] = j - 1
+    iota(A("J", 0, 144), [[1, 144]], 0, -1)
+    iota(A("K", 0, 128), [[16, 8], [0, 16]], 0, -1)
+    iota(full("pos2"), [[2, V]], 0, 0)
+    i = share("T0", 0, V, "arr0", "sent0", 1500.0)
+    load("y", full("thi"), T.th[:], "ldt", 1100.0, also=[i])
+    iota(A("RM", 0, 16 * CH), [[0, 4 * CH], [256, 4]], 0, 0)
+    tasks[-1]["behind"] = i
+
+    JS = A("J", 0, 128)
+    fill(A("half", 0, 128, parts=1), 0.5)
+    fill(A("c192", 0, 128, parts=1), 192.0)
+    fill(A("c256", 0, 256, parts=1), 256.0)
+    fill(A("zero", 0, 128, parts=1), 0.0)
+    fill(A("en", 0, 144), 0.0)
+    ts(HEYE, JS, 0.0, -HUGE, ALU.is_equal, ALU.mult)
+    ts(A("jge", 0, 128), JS, 0.0, None, ALU.is_ge)
+    fill(A("en", 15, 144, 16), -1.0)
+    ts(EYE, JS, 0.0, None, ALU.is_equal)
+    ts(NEYE, JS, 0.0, -1.0, ALU.is_equal, ALU.mult)
+    ts(EYE16, JS, 0.0, None, ALU.is_equal)
+    ts(A("j1", 0, 128), JS, 1.0, None, ALU.is_equal)
+    ts(A("k0", 0, 128), A("K", 0, 128), 0.0, None, ALU.is_equal)
+    act(A("zs", 0, 128), A("K", 0, 128), ACT.Sigmoid, bias=128.0, scale=-256.0, more=1300.0)
+    task("v", lambda: g.vector.tensor_reduce(T.pm0[:, 0:1], T.k0[:, 0:128], AxisListType.X, ALU.max), [("k0", 0, 128)], [("pm0", 0, 1)], 190.0)
+    cp(L1, A("rfi", 0, 32))
+    ts(A("l1a", 0, 32), A("rfi", 0, 32), 2.0, 1.0, ALU.mult, ALU.add)
+    ts(A("wsel", 0, 144), A("J", 0, 144), 15.0, A("pm0", 0, 1), ALU.is_equal, ALU.mult)
+    tt(A("tri16", 0, 128), A("jge", 0, 128), A("zs", 0, 128), ALU.mult)
+    tt(TRI, A("jge", 0, 128), A("zs", 0, 128), ALU.mult)
+    tt(A("j1", 0, 128), A("j1", 0, 128), A("zs", 0, 128), ALU.mult)
+    tt(BD, EYE, A("j1", 0, 128), ALU.subtract)
+    for bank in ("D0", "D1"):
+        mm(full(bank), A("half", 0, 128, parts=1), A("pos2", 0, V, parts=1), True, False)
+    act(full("r1"), ind(full("pos2"), L1), ACT.Copy)
+    ts(full("ownb"), full("cpi"), -1.0, 1.0, ALU.mult, ALU.add)
+    act(full("cpb"), full("ownb"), ACT.Identity, bias=1.0, scale=-1.0)
+    tt(full("og"), full("gpi"), full("ownb"), ALU.mult)
+    act(A("r23", 0, V), ind(full("r1"), L1), ACT.Copy)
+    mm(full("D1"), HEYE, full("cpb"), False, False)
+    mm(full("D1"), A("tri16", 0, 128), full("og"), False, True)
+    mm(full("D0"), A("tri16", 0, 128), full("og"), False, True)
+    act(full("u1"), full("D1"), ACT.Relu, bias=float(own + BIG))
+    ts(full("x0"), full("D0"), float(own), None, ALU.add)
+    act(full("u2"), full("D1"), ACT.Relu, bias=float(own + 2 * BIG))
+    act(full("u3"), full("D1"), ACT.Relu, bias=float(own + 3 * BIG))
+    act(A("r23", V, 2 * V), ind(A("r23", 0, V), L1), ACT.Copy)
+    tt(full("x1"), ind(full("x0"), L1), full("u1"), ALU.max)
+    tt(full("x2"), ind(full("x1"), L1), full("u2"), ALU.max)
+    R0 = OPT["r0"]
+    for lo, hi in ((0, R0), (R0, V)):
+        tt(A("x3", lo, hi), ind(full("x2"), A("l1", lo // 16, hi // 16)), A("u3", lo, hi), ALU.max)
+        ts(A("x3", lo, hi), A("x3", lo, hi), 4095, None, ALU.bitwise_and)
+        cp(A("soff", lo, hi), A("x3", lo, hi))
+    for q in range(16):
+        mm(A("CM", 0, 64), A("wsel", 15 - q, 143 - q), A("r23", q, 2 * V, 16), q == 0, q == 15)
+    ts(A("l23", 0, 32), A("CM", 0, 32), 1.0, None, ALU.add)
+    ts(A("l23", 32, 64), A("CM", 32, 64), 0.0, None, ALU.add)
+    cp(full("thb"), full("thi"))
+    ts(A("eyeh", 0, 128), JS, 0.0, 0.5, ALU.is_equal, ALU.mult)
+    act(full("cp1"), ind(full("cpb"), L1), ACT.Copy, scale=0.5)
+    act(full("cp2"), ind(full("cp1"), L1), ACT.Copy, scale=0.5)
+    for j, name in enumerate(("cpb", "cp1", "cp2")):
+        mm(full("F1"), EYE, full(name), j == 0, j == 2)
+    act(full("kst"), full("F1"), ACT.Identity, bias=1.0 / 32, scale=0.25)
+
+    def mine(r, lo, hi):
+        return A("T%d" % r, own + lo, own + hi)
+
+    def gather(r, lo, hi, on_v):
+        src = ind(A("T%d" % r, 0, 4096 + (2 if r else 0)), A("soff", lo, hi))
+        if on_v:
+            cp(A("P", 16 * lo, 16 * hi), src)
+        else:
+            act(A("P", 16 * lo, 16 * hi), src, ACT.Copy)
+
+    def sets(c):
+        return (c[1] - c[0]) // 32
+
+    def scan(c):
+        p, m, rm = A("P", 16 * c[0], 16 * c[1]), A("M", 16 * c[0], 16 * c[1]), A("RM", 0, 16 * (c[1] - c[0]))
+        task("v", lambda: g.vector.tensor_tensor_scan(m[0], rm[0], p[0], 0.0, ALU.min, ALU.max), regs(p, rm), regs(m), price(m, p, 0.5))
+
+    def crep(r, c, bank):
+        rep = 16 // sets(c)
+        for j in range(rep):
+            mm(A(bank, j, 512, rep), EYE, mine(r, *c), True, True)
+
+    def links(c, s):
+        return A("P", 16 * c[0] + s, 16 * c[1], sets(c))
+
+    def bits(c, s):
+        return A("B", 16 * c[0] + 512 * s, 16 * c[0] + 512 * (s + 1))
+
+    def compare(c, s, bank):
+        tt(bits(c, s), links(c, s), full(bank), ALU.is_gt)
+
+    def compare_s(r, c, s, bank, early):
+        rep = 16 // sets(c)
+        if early:
+            mm(full(bank), A("zero", 0, 128, parts=1), A("ownb", 0, V, parts=1), True, False)
+        else:
+            mm(full(bank), EYE, links(c, s), True, False)
+        for j in range(rep):
+            mm(A(bank, j, 512, rep), NEYE, mine(r, *c), False, j == rep - 1 and not early)
+        if early:
+            mm(full(bank), EYE, links(c, s), False, True)
+        step(bits(c, s), full(bank))
+
+    def count(r, c, bank, ss):
+        rep = 16 // sets(c)
+        f = A(bank, *c)
+        late = r == 0 and c[0] == 0
+        mm(f, HEYE, A("cpb", *c), True, False)
+        if not late:
+            mm(f, EYE, A("thb", *c), False, False)
+        for s in ss:
+            for j in range(rep):
+                k = sets(c) * j + s
+                lo = 16 * c[0] + 512 * s
+                mm(f, A("en", 15 - k, 143 - k), A("B", lo + j, lo + 512, rep), False, s == ss[-1] and j == rep - 1 and not late)
+        if late:
+            mm(f, EYE, A("thb", *c), False, True)
+
+    def sums(r, c):
+        x = A("X", *c)
+        mm(x, A("c192", 0, 128, parts=1), A("c256", 0, c[1] - c[0], parts=1), True, False)
+        mm(x, EYE, mine(r, *c), False, False)
+        for b in range(4):
+            mm(x, EYE, A("M", 16 * c[0] + 4 * b + 3, 16 * c[1], 16), False, b == 3)
+
+    def registers(r, lo, hi, tag):
+        if tag in OPT["rounds"][r]["high_v"]:
+            ts(A("yq", lo, hi), A("X", lo, hi), -127.5, None, ALU.add)
+        else:
+            act(A("yq", lo, hi), A("X", lo, hi), ACT.Identity, bias=-127.5)
+        tt(mine(r + 1, lo, hi) if r < 2 else A("cout", lo, hi), A("X", lo, hi), A("yq", lo, hi), ALU.subtract)
+        if r < 2:
+            return share("T%d" % (r + 1), lo, hi, "arr%d%s" % (r + 1, tag), "sent")
+        store(T.yc[:, lo:hi], A("cout", lo, hi), 500.0)
+
+    def running(r, lo, hi, bank):
+        step(A("mb", lo, hi), A(bank, lo, hi))
+        n = hi - lo
+        if r < 2:
+            mm(A("CM", 1, 2 * n, 2), HEYE, A("cpb", lo, hi), True, False)
+            mm(A("CM", 1, 2 * n, 2), TRI, A("mb", lo, hi), False, True)
+            mm(A("CM", 0, 2 * n, 2), TRI, A("mb", lo, hi), True, True)
+            step(A("W%d" % r, 2 * lo, 2 * hi), A("CM", 0, 2 * n))
+        else:
+            mm(A("CM", 0, n), TRI, A("mb", lo, hi), True, True)
+            step(A("W2", lo, hi), A("CM", 0, n))
+
+    def shift(r, lo, hi, bank, by):
+        mm(A(bank, lo, hi), EYE16, A("s16", lo, hi), True, False)
+        mm(A(bank, lo, hi), EYE, A("kst", lo, hi), False, False)
+        mm(A(bank, lo, hi), A("eyeh", 0, 128), A("W%d" % r, 2 * lo + 1, 2 * hi, 2), False, False)
+        for j, (lst, at) in enumerate((("l1a", 0), ("l23", 0), ("l23", 32))):
+            t = A("t%d" % (j + 1), lo, hi)
+            src = ind(A("W%d" % r, 0, 2 * V), A(lst, at + lo // 16, at + hi // 16))
+            if by[j] == "v":
+                ts(t, src, 0.25 / 2 ** j, None, ALU.mult)
+            else:
+                act(t, src, ACT.Copy, scale=0.25 / 2 ** j)
+            mm(A(bank, lo, hi), EYE, t, False, j == 2)
+        ts(A("soff", lo, hi), A(bank, lo, hi), ROUND, ROUND - 2048.0, ALU.add, ALU.subtract)
+
+    def gaps(lo, hi, bank):
+        mm(A(bank, lo, hi), BD, A("W0", 2 * lo, 2 * hi, 2), True, False)
+        mm(A(bank, lo, hi), BD, A("W1", 2 * lo, 2 * hi, 2), False, False)
+        mm(A(bank, lo, hi), BD, A("W2", lo, hi), False, True)
+        tt(A("gout", lo, hi), A(bank, lo, hi), A("gpi", lo, hi), ALU.add)
+        store(T.yg[:, lo:hi], A("gout", lo, hi), 280.0 + 1.6 * (hi - lo))
+
+    for r in range(3):
+        o = OPT["rounds"][r]
+        cuts = o["cuts"]
+        chunks = list(zip(cuts[:-1], cuts[1:]))
+        for lo, hi in zip(o["gathers"][:-1], o["gathers"][1:]):
+            gather(r, lo, hi, lo in o["by_v"])
+            if lo not in o["by_v"]:
+                if lo:
+                    tasks[-1]["behind"] = prev
+                prev = len(tasks) - 1
+        if r < 2:
+            ts(full("s16"), full("soff"), -2048.0, None, ALU.add)
+        sent, first, n_d, n_c = 0, None, 0, 0
+        n0 = len(tasks)
+        for c in zip(o["scans"][:-1], o["scans"][1:]):
+            scan(c)
+            sums(r, c)
+            if c[1] in o["sends"]:
+                i = registers(r, sent, c[1], "abc"[o["sends"].index(c[1])])
+                first, sent = (i if first is None else first), c[1]
+        for t in tasks[n0:]:
+            t["boost"] = o["boost"]
+        if r < 2:
+            t = "T%d" % (r + 1)
+            task("g", lambda t=t: g.affine_select(T[t][:, 4096:4098], T[t][:, 0:2], [[0, 2]], ALU.is_ge, 0.0, 0, 0),
+                 [(t, 0, 2)], [(t, 4096, 4098)], 170.0, also=[first + 1])
+            tasks[-1]["behind"] = i
+        for j in o["order"]:
+            c = chunks[j]
+            n_s = o["by_s"][j]
+            for s in range(n_s):
+                banks = o["banks"]
+                compare_s(r, c, s, banks[n_d % len(banks)], n_d < len(banks))
+                n_d += 1
+            if n_s < sets(c):
+                crep(r, c, "CR%d" % (n_c % 2))
+                for s in range(n_s, sets(c)):
+                    compare(c, s, "CR%d" % (n_c % 2))
+                n_c += 1
+            count(r, c, o["fbank"][j], list(range(sets(c))))
+            if j == 1:
+                running(r, 0, c[1], "F0")
+            elif j > 1:
+                running(r, c[0], c[1], o["fbank"][j])
+        if r < 2:
+            for j, (lo, hi, by) in enumerate(OPT["shifts"]):
+                shift(r, lo, hi, ["D1", "D0", "CR0"][j], by)
+        else:
+            for j, (lo, hi) in enumerate(zip(o["gaps"][:-1], o["gaps"][1:])):
+                gaps(lo, hi, ["D1", "D0"][j % 2])
+
+    if "seq" not in PLAN:
+        plan = [dict(t) for t in tasks]
+        for t in plan:
+            if "behind" in t:
+                t["deps"] = sorted(set(t["deps"] + [t["behind"]]))
+        PLAN["seq"] = OPT.get("arrange", arrange)(plan)
+    known = {q: {} for q in queue}
+    total = {}
+    mark = {}
+
+    def wait(q, sem, count, seen):
+        if known[q].get(sem, 0) >= count:
+            return
+        queue[q].wait_ge(T.sem[sem], count)
+        known[q][sem] = count
+        for s, c in seen.items():
+            if known[q].get(s, 0) < c:
+                known[q][s] = c
+
+    for i in PLAN["seq"]:
+        t = tasks[i]
+        q = t["q"]
+        if q == "far":
+            mark[i] = (t["sem"], t["count"], {})
+            continue
+        need = {}
+        for d in t["deps"]:
+            if q == "p" and tasks[d]["q"] == "p":
+                continue
+            sem, count, seen = mark[d]
+            if count > need.get(sem, (0, None))[0]:
+                need[sem] = (count, seen)
+        for sem in sorted(need, key=lambda s: s == COUNTER.get(q)):
+            wait(q, sem, need[sem][0], need[sem][1])
+        ins = t["call"]()
+        sem, count = (t["sem"], t["count"]) if t["sem"] else (COUNTER[q], 1)
+        if ins is not None:
+            ins.then_inc(T.sem[sem], count)
+        total[sem] = total.get(sem, 0) + count
+        mark[i] = (sem, total[sem], dict(known[q]))
+    wait("g", "sent", total["sent"], {})
+    for sem in ("qv", "qs", "qp", "qg", "st"):
+        wait("y", sem, total[sem], {})

@@ -43,9 +43,9 @@ PSUM = [k for k in SCRATCH if SCRATCH[k][0] == "psum"]
 SEMAPHORES = ["qv", "qs", "qp", "qg", "ldc", "ldg", "ldp", "ldr", "ldt", "arr0", "arr1a", "arr1b", "arr1c", "arr2a", "arr2b", "arr2c",
               "sent0", "sent", "st"]
 COUNTER = {"v": "qv", "s": "qs", "p": "qp", "g": "qg"}
-OPT = {"r0": 128,
-       "shifts": [(0, 128, "vsv"), (128, 256, "svs"), (256, 512, "vss")],
-       "rounds": [{"cuts": [0, 128, 256, 384, 512], "gathers": [0, 64, 128, 256, 384, 512], "by_v": [64], "high_v": ["a", "a", ""][r],
+OPT = {"r0": [0, 128, 512], "tt2": 1.0,
+       "shifts": [(0, 128, "vss"), (128, 512, "sss")],
+       "rounds": [{"cuts": [0, 128, 256, 384, 512], "gathers": [0, 64, 128, 256, 384, 512], "by_v": [64], "ct": "v", "high_v": "",
                    "scans": [0, 128, 256, 384, 512],
                    "sends": [[256, 512], [256, 512], [384, 512]][r], "order": [0, 1, 2, 3], "by_s": [0, 0, 0, [2, 2, 3][r]],
                    "banks": ["D0", "D1"], "fbank": ["F0", "F0", "F1", "F0"], "gaps": [0, 384, 512],
@@ -55,7 +55,7 @@ PLAN = {}
 
 
 ORDER = (
-    "00040b010d02030c060j1r0k0h0f0g0i0e0l050y1d0n0o0p070s0x0m0a0A2r2s2t0q2u210t220z23240u1s0C0B0D0E290r0F0v0G0H1g0I0J0M3r0K3s3t3u3v1e0N3y3z3A3B3C0L1h0O0R1f0U0P080V090S0W0X0Y0Q0Z0T101k11121l131415161i171m18191q251t1u1v1w1y1z262a2b2c2d1n272e2f2g2h1x2i2j2k2l281A1B1C1D1c2W2m2n2X2Y1j2o1E2p2q2z2Z2v2A1o34351F2B2C2D1I2E1G1J1K2w1L1M1N1O1Q1R2x2F2G2H2I2y2J2K2L2M1P2N2O2P2Q3D2R3w3E3F3L301S1T1U1V3G1W3M1b361H1a373x2S1X3839313H1Y3I3N3O3P3Q323a203b3c3d2T333e3f3g2U3R2V3J3h3S3T3U3i3j3k3K3n3l3V3m3W3X3Y1p3o3p3Z3q400w41424843444945464a474i4j4s4t4d4f4u1Z4b4l4k4J5r4n4z4c4e4v4g4m4p4o5s5J4h4x4w4q4D5K4C4y4A5L5M6m4K6Q6R6S6T4r6n6U4B4E6J4I5j5k5l5m6K6L6M6N6a5n4L4M4N4O4Q4R5o5t5u5v5w5p5x5y4F5z5A4P5B5C5D5E5q4S4T4U4V4W5F5G5H5N5I5R6e6f4G5S6g6h4X5T5U5V505W4Y51525O5354555658595P5X5Y5Z605Q6162636457656667686O696X6Y6P6Z73706i5a5b5c5d6V5e4H4Z6o6p6W6q5f6r6b6j6c5g746d757677786k6s5i6t6u6v6F796l6w6x6y6z7a7b716A6B6C6D7c6E7q727d6G6H7e6I7f7g7h7i7j7k7m7l7r7s7n7o7A7p7B7C7K7L7t7v7M7x7D7u5h7w7H7N7y7E7P809y7z7O7F7R7Q7V7G7I7U7S8F9z8Ga08Xa1a2a3a47J818Y7T8Z7W907Z8x8y8z8A9T9U9V9W9X8B8283848587888D8H8I8J8K8C7X8E8L8M8N8O8P8Q929q9r9s9t8R8S918T8U8V8W9596949798999a9b9c937Y9d9e86adaeafag9f9g9h9i9j9k9l9m9u898a8b8c8e8f8d9A9B9C9D9na59oa6aiaj9v9Y8g9Z8h8i9w9E9F9G9HaD9p9x9I9J9K8j9L8kak8n9Ma79N9O9Pa89Qa9aaabaEahac9Ralamanao8l9SapaqarasaF8mataGauavawaxayazaH8oaA8p8q8r8s8taB8uaIaJaC8vaK8waLaM"
+    "0001060c02030b040d050f0o1r0e0i070g0h0n0p0s0j0y0t0A0u0x0B080q0C0z0a0E292r1e1s1c0G0F0I2a0H1g1h0k210J220M3r23240K2s3s2t3t0N2u3u1f3v3y3z3A3B3C0O0D1i0P0R090L0Q0S1k1l0U0V0W0X0Y0Z101112131j0T1415161q171m18193435261t1u1v1w1y1z2728251n1b2b1a2c1x2d2S2e2f2g2h2i2j2k2l2W2m2x1A1B1C1D2n2o2v2p2q2z2A2X2Y2Z2w2B1o2C2D2E2y2F2G2H2I2J2K303F3G2L2M3H3I3136372N2O2P2Q3238393a3b3c3d333e3f1E3g3h2R1I3i3j3k3l3w3m3D3x2T1F2U3L3E3M1P1G1J1K1L1M1N1O2V1Q1R3N3O3P3Q3J1S1T1U1V3n3o1W3K3p3R3S3q3T3U3V3W1X3X3Y3Z1p401Y4142440l59435a1H0r5b1d4546200m4849474a4i4j4b4p5c0v4c4k4d5h0w5i6c4f4e6d4n4g5z4z4h5A5B5C4l601Z4A6G4t6H4s4m4o4q6I6J6K4r4y4u6z6A6B6C6D5f4B4C4D4E4G4H5e5g5d4v5E5j5k5l5m64654F5n5o5p5q66675r5s5t5u5v5w5x5D5y5H5I4I4J4K5G4L5J5K5L4w5M5N5O5F5P5Q686N5R5S5T5U5V696e6f6g6h5W5X4Q6i6j6k6l5Y6O6P6Q4M6E4X5Z6L6F61626T6U4N636V6W6X6a6Y4O4R4S6M4T6v4U6b4V4W4Y6m6n6o6p6R4Z6q6r6s6t50516u6S52536Z70547172737455756w6x764x776y5678794P7a7c7b7q587d7e7r7f7g7h7i7j7n7s8d7l7k8e7x7m7o8f8g7p9e9f7t7G7H8D8E8F8l578G7v7u7B8m9G7A7w7y9H9I9J9K7z8j7C9z9A9B9C8i9D7F8k7I7J7K7L7N7O8h7D8H968n8o978p8q7M988r8s8t998u8v8w8x8y8z8A8B8K7P8C8L8M8N8O8I8P8Q7Q7R7E7S7U7V8J8R8S8T8U9a9T9U9V9W8V8W9b8X8Y9g9h9i8Z909c9j9k9l9m9n919d929o9p9q9r939E7T9L9F9s9t9Y9u9v9M9N839O7W949w9P9Q959R7X7Y9Saj9X7Zak9Z80a0a1a2a39xa481a59ya6a7a8a9aa82abacadaeafalag8485am8687ah8889aiaoanap8aaqar8bas8c"
 )
 
 
@@ -130,7 +130,7 @@ def rank_program(g, core, T, topo):
         task("v", call, regs(a, s1, s2), regs(out), price(out, a, narrow(out, a)))
 
     def tt(out, a, b, o):
-        k = 1.0 if a[1][0] in PSUM or b[1][0] in PSUM else 2.0
+        k = (1.0 if a[1][0] in PSUM or b[1][0] in PSUM else 2.0) * (OPT["tt2"] if narrow(out, a, b) < 1 else 1.0)
         task("v", lambda: g.vector.tensor_tensor(out[0], a[0], b[0], o), regs(a, b), regs(out), price(out, a, k))
 
     def cp(out, a):
@@ -187,15 +187,15 @@ def rank_program(g, core, T, topo):
         return A(name, 0, V)
 
     i = load("y", A("T0", own, own + V), T.c0[:], "ldc", 700.0)
-    for out, src, sem, busy in ((A("rfi", 0, 32), T.rf[:], "ldr", 330.0), (full("cpi"), T.cp[:], "ldp", 1100.0),
-                                (full("gpi"), T.gp[:], "ldg", 1100.0)):
-        j = load("y", out, src, sem, busy)
-        tasks[j]["behind"] = j - 1
+    load("s", full("cpi"), T.cp[:], "ldp", 1100.0)
+    for q, out, src, sem, busy in (("y", full("gpi"), T.gp[:], "ldg", 1100.0), ("s", A("rfi", 0, 32), T.rf[:], "ldr", 330.0),
+                                   ("y", full("thi"), T.th[:], "ldt", 1100.0)):
+        j = load(q, out, src, sem, busy)
+        tasks[j]["behind"] = j - 2
     iota(A("J", 0, 144), [[1, 144]], 0, -1)
     iota(A("K", 0, 128), [[16, 8], [0, 16]], 0, -1)
     iota(full("pos2"), [[2, V]], 0, 0)
-    i = share("T0", 0, V, "arr0", "sent0", 1500.0)
-    load("y", full("thi"), T.th[:], "ldt", 1100.0, also=[i])
+    i = share("T0", 0, V, "arr0", "sent", 1500.0)
     iota(A("RM", 0, 16 * CH), [[0, 4 * CH], [256, 4]], 0, 0)
     tasks[-1]["behind"] = i
 
@@ -240,7 +240,7 @@ def rank_program(g, core, T, topo):
     tt(full("x1"), ind(full("x0"), L1), full("u1"), ALU.max)
     tt(full("x2"), ind(full("x1"), L1), full("u2"), ALU.max)
     R0 = OPT["r0"]
-    for lo, hi in ((0, R0), (R0, V)):
+    for lo, hi in zip(R0[:-1], R0[1:]):
         tt(A("x3", lo, hi), ind(full("x2"), A("l1", lo // 16, hi // 16)), A("u3", lo, hi), ALU.max)
         ts(A("x3", lo, hi), A("x3", lo, hi), 4095, None, ALU.bitwise_and)
         cp(A("soff", lo, hi), A("x3", lo, hi))
@@ -262,21 +262,24 @@ def rank_program(g, core, T, topo):
     def gather(r, lo, hi, on_v):
         src = ind(A("T%d" % r, 0, 4096 + (2 if r else 0)), A("soff", lo, hi))
         if on_v:
-            cp(A("P", 16 * lo, 16 * hi), src)
+            cp(gathered(lo, hi), src)
         else:
-            act(A("P", 16 * lo, 16 * hi), src, ACT.Copy)
+            act(gathered(lo, hi), src, ACT.Copy)
 
     def sets(c):
         return (c[1] - c[0]) // 32
 
     def scan(c):
-        p, m, rm = A("P", 16 * c[0], 16 * c[1]), A("M", 16 * c[0], 16 * c[1]), A("RM", 0, 16 * (c[1] - c[0]))
+        p, m, rm = gathered(*c), A("M", 16 * c[0], 16 * c[1]), A("RM", 0, 16 * (c[1] - c[0]))
         task("v", lambda: g.vector.tensor_tensor_scan(m[0], rm[0], p[0], 0.0, ALU.min, ALU.max), regs(p, rm), regs(m), price(m, p, 0.5))
 
     def crep(r, c, bank):
         rep = 16 // sets(c)
         for j in range(rep):
             mm(A(bank, j, 512, rep), EYE, mine(r, *c), True, True)
+
+    def gathered(lo, hi):
+        return A("P", 16 * lo, 16 * hi)
 
     def links(c, s):
         return A("P", 16 * c[0] + s, 16 * c[1], sets(c))
@@ -302,7 +305,7 @@ def rank_program(g, core, T, topo):
     def count(r, c, bank, ss):
         rep = 16 // sets(c)
         f = A(bank, *c)
-        late = r == 0 and c[0] == 0
+        late = False
         mm(f, HEYE, A("cpb", *c), True, False)
         if not late:
             mm(f, EYE, A("thb", *c), False, False)
@@ -396,7 +399,7 @@ def rank_program(g, core, T, topo):
             n_s = o["by_s"][j]
             for s in range(n_s):
                 banks = o["banks"]
-                compare_s(r, c, s, banks[n_d % len(banks)], n_d < len(banks))
+                compare_s(r, c, s, banks[n_d % len(banks)], s < len(banks))
                 n_d += 1
             if n_s < sets(c):
                 crep(r, c, "CR%d" % (n_c % 2))
@@ -410,7 +413,7 @@ def rank_program(g, core, T, topo):
                 running(r, c[0], c[1], o["fbank"][j])
         if r < 2:
             for j, (lo, hi, by) in enumerate(OPT["shifts"]):
-                shift(r, lo, hi, ["D1", "D0", "CR0"][j], by)
+                shift(r, lo, hi, ["D1", "D0", "F1"][j], by)
         else:
             for j, (lo, hi) in enumerate(zip(o["gaps"][:-1], o["gaps"][1:])):
                 gaps(lo, hi, ["D1", "D0"][j % 2])

@@ -1,69 +1,145 @@
+import math
 from concourse.bass import DstId, RemoteDMATransfer
 from concourse.mybir import AluOpType as ALU, AxisListType, ActivationFunctionType as ACT
 
 V = 512
-CH = 128
 TW = 4096 + 16
-HUGE = 1048576.0
+HUGE = 4194304.0
 ROUND = 12582912.0
-BIG = 40960.0
+BIG = 262144.0
 
-SCRATCH = {
-    "T0": ("sbuf", [128, TW], "bfloat16"), "T1": ("sbuf", [128, TW], "bfloat16"), "T2": ("sbuf", [128, TW], "bfloat16"),
-    "cout": ("sbuf", [128, V], "bfloat16"), "gout": ("sbuf", [128, V], "float32"),
-    "gpi": ("sbuf", [128, V], "int32"), "cpi": ("sbuf", [128, V], "int32"), "thi": ("sbuf", [128, V], "int32"),
-    "rfi": ("sbuf", [128, 32], "int32"),
-    "P": ("sbuf", [128, 16 * V], "bfloat16"), "M": ("sbuf", [128, 16 * V], "bfloat16"), "B": ("sbuf", [128, 16 * V], "bfloat16"),
-    "RM": ("sbuf", [128, 16 * CH], "bfloat16"),
-    "J": ("sbuf", [128, 144], "float32"), "K": ("sbuf", [128, 128], "float32"), "pos2": ("sbuf", [128, V], "float32"),
-    "eye": ("sbuf", [128, 128], "bfloat16"), "neye": ("sbuf", [128, 128], "bfloat16"), "heye": ("sbuf", [128, 128], "bfloat16"),
-    "eye16": ("sbuf", [128, 128], "float16"), "zs": ("sbuf", [128, 128], "bfloat16"), "jge": ("sbuf", [128, 128], "bfloat16"),
-    "tri": ("sbuf", [128, 128], "bfloat16"), "tri16": ("sbuf", [128, 128], "float16"), "bd": ("sbuf", [128, 128], "bfloat16"),
-    "j1": ("sbuf", [128, 128], "bfloat16"), "k0": ("sbuf", [128, 128], "float32"), "pm0": ("sbuf", [128, 8], "float32"),
-    "wsel": ("sbuf", [128, 144], "float32"), "en": ("sbuf", [128, 144], "bfloat16"),
-    "half": ("sbuf", [128, 128], "float32"), "c192": ("sbuf", [128, 128], "bfloat16"), "c256": ("sbuf", [128, 256], "bfloat16"),
-    "zero": ("sbuf", [128, 128], "bfloat16"),
-    "l1": ("sbuf", [128, 32], "uint16"), "l1a": ("sbuf", [128, 32], "uint16"), "l23": ("sbuf", [128, 64], "uint16"),
-    "r1": ("sbuf", [128, V], "float32"), "r23": ("sbuf", [128, 2 * V], "float32"),
-    "ownb": ("sbuf", [128, V], "bfloat16"), "cpb": ("sbuf", [128, V], "bfloat16"), "thb": ("sbuf", [128, V], "bfloat16"),
-    "og": ("sbuf", [128, V], "float16"), "cp1": ("sbuf", [128, V], "bfloat16"), "cp2": ("sbuf", [128, V], "bfloat16"),
-    "kst": ("sbuf", [128, V], "bfloat16"), "eyeh": ("sbuf", [128, 128], "bfloat16"),
-    "x0": ("sbuf", [128, V], "float32"), "x1": ("sbuf", [128, V], "float32"), "x2": ("sbuf", [128, V], "float32"),
-    "x3": ("sbuf", [128, V], "int32"),
-    "u1": ("sbuf", [128, V], "float32"), "u2": ("sbuf", [128, V], "float32"), "u3": ("sbuf", [128, V], "float32"),
-    "soff": ("sbuf", [128, V], "uint16"), "s16": ("sbuf", [128, V], "float16"),
-    "yq": ("sbuf", [128, V], "bfloat16"), "mb": ("sbuf", [128, V], "bfloat16"),
-    "W0": ("sbuf", [128, 2 * V], "bfloat16"), "W1": ("sbuf", [128, 2 * V], "bfloat16"), "W2": ("sbuf", [128, V], "bfloat16"),
-    "t1": ("sbuf", [128, V], "bfloat16"), "t2": ("sbuf", [128, V], "bfloat16"), "t3": ("sbuf", [128, V], "bfloat16"),
-    "CR0": ("psum", [128, 512], "float32"), "CR1": ("psum", [128, 512], "float32"), "X": ("psum", [128, 512], "float32"),
-    "F0": ("psum", [128, 512], "float32"), "F1": ("psum", [128, 512], "float32"), "CM": ("psum", [128, 512], "float32"),
-    "D0": ("psum", [128, 512], "float32"), "D1": ("psum", [128, 512], "float32"),
+BF, F16, F32, I32, U16 = "bfloat16", "float16", "float32", "int32", "uint16"
+SBUF = {
+    "T0": (TW, BF), "T1": (TW, BF), "T2": (TW, BF), "cout": (V, BF), "gout": (V, F32),
+    "gpi": (V, I32), "cpi": (V, I32), "thi": (V, I32), "rfi": (32, I32),
+    "P": (16 * V, BF), "M": (16 * V, BF), "B": (16 * V, BF), "C8": (8 * V, BF), "RM": (2048, BF),
+    "J": (144, F32), "K": (128, F32), "pos": (V, BF),
+    "eye": (128, BF), "neye": (128, BF), "heye": (128, BF), "eye5": (128, BF), "zs": (128, BF), "jge": (128, BF),
+    "tri": (128, BF), "fw": (128, BF), "fm": (128, BF), "sel": (512, BF), "en": (144, BF), "spread": (1024, BF), "fts": (64, BF),
+    "k0": (128, F32), "pm0": (8, F32), "wsel": (144, BF), "cm": (128, BF), "ch": (128, BF), "zero": (128, BF), "ones": (V, BF),
+    "l1": (32, U16), "l23": (64, U16), "r1": (V, BF), "r23": (2 * V, BF),
+    "cpb": (V, BF), "thc": (V, BF), "og": (V, F16), "cp1": (V, BF), "cp2": (V, BF), "kst": (V, BF), "amp": (V, BF),
+    "x0": (V, F32), "x1": (V, F32), "x2": (V, F32), "x3": (V, I32), "x4": (V, I32), "u1": (V, F32), "u2": (V, F32), "u3": (V, F32),
+    "soff": (V, U16), "s0": (V, F16), "s16": (V, F16), "yq": (V, BF),
+    "inc0": (V, BF), "inc1": (V, BF), "mb0": (V, BF), "mb1": (V, BF), "mb2": (V, BF), "y": (V, BF), "t1": (V, BF), "t2": (V, BF), "t3": (V, BF),
 }
-PSUM = [k for k in SCRATCH if SCRATCH[k][0] == "psum"]
+PSUM = ["D0", "D1", "D2", "X", "FT", "F", "CM", "S0"]
+SCRATCH = {k: ("sbuf", [128, SBUF[k][0]], SBUF[k][1]) for k in SBUF}
+SCRATCH.update({k: ("psum", [128, 512], F32) for k in PSUM})
 SEMAPHORES = ["qv", "qs", "qp", "qg", "ldc", "ldg", "ldp", "ldr", "ldt", "arr0", "arr1a", "arr1b", "arr1c", "arr2a", "arr2b", "arr2c",
-              "sent0", "sent", "st"]
+              "sent", "st"]
 COUNTER = {"v": "qv", "s": "qs", "p": "qp", "g": "qg"}
-OPT = {"r0": [0, 128, 512], "tt2": 1.0,
-       "shifts": [(0, 128, "vss"), (128, 512, "sss")],
-       "rounds": [{"cuts": [0, 128, 256, 384, 512], "gathers": [0, 64, 128, 256, 384, 512], "by_v": [64], "ct": "v", "high_v": "",
-                   "scans": [0, 128, 256, 384, 512],
-                   "sends": [[256, 512], [256, 512], [384, 512]][r], "order": [0, 1, 2, 3], "by_s": [0, 0, 0, [2, 2, 3][r]],
-                   "banks": ["D0", "D1"], "fbank": ["F0", "F0", "F1", "F0"], "gaps": [0, 384, 512],
-                   "boost": [6000.0, 6000.0, 0.0][r]} for r in range(3)],
-       "g": 1.3, "e": 1.04, "pe": 0.53, "hop": 80.0}
-PLAN = {}
 
+PART = {"A1": (0, 128), "B1": (128, 256), "B2": (256, 384), "A2": (384, 512), "a": (0, 256), "b": (256, 512), "all": (0, 512),
+        "A1x": (0, 64), "A1y": (64, 128), "B1x": (128, 192), "B1y": (192, 256), "B2x": (256, 320), "B2y": (320, 384),
+        "A2x": (384, 448), "A2y": (448, 512), "c": (0, 384), "B": (128, 384)}
+ON_VECTOR = (0, 384)
 
-ORDER = (
-    "0001060c02030b040d050f0o1r0e0i070g0h0n0p0s0j0y0t0A0u0x0B080q0C0z0a0E292r1e1s1c0G0F0I2a0H1g1h0k210J220M3r23240K2s3s2t3t0N2u3u1f3v3y3z3A3B3C0O0D1i0P0R090L0Q0S1k1l0U0V0W0X0Y0Z101112131j0T1415161q171m18193435261t1u1v1w1y1z2728251n1b2b1a2c1x2d2S2e2f2g2h2i2j2k2l2W2m2x1A1B1C1D2n2o2v2p2q2z2A2X2Y2Z2w2B1o2C2D2E2y2F2G2H2I2J2K303F3G2L2M3H3I3136372N2O2P2Q3238393a3b3c3d333e3f1E3g3h2R1I3i3j3k3l3w3m3D3x2T1F2U3L3E3M1P1G1J1K1L1M1N1O2V1Q1R3N3O3P3Q3J1S1T1U1V3n3o1W3K3p3R3S3q3T3U3V3W1X3X3Y3Z1p401Y4142440l59435a1H0r5b1d4546200m4849474a4i4j4b4p5c0v4c4k4d5h0w5i6c4f4e6d4n4g5z4z4h5A5B5C4l601Z4A6G4t6H4s4m4o4q6I6J6K4r4y4u6z6A6B6C6D5f4B4C4D4E4G4H5e5g5d4v5E5j5k5l5m64654F5n5o5p5q66675r5s5t5u5v5w5x5D5y5H5I4I4J4K5G4L5J5K5L4w5M5N5O5F5P5Q686N5R5S5T5U5V696e6f6g6h5W5X4Q6i6j6k6l5Y6O6P6Q4M6E4X5Z6L6F61626T6U4N636V6W6X6a6Y4O4R4S6M4T6v4U6b4V4W4Y6m6n6o6p6R4Z6q6r6s6t50516u6S52536Z70547172737455756w6x764x776y5678794P7a7c7b7q587d7e7r7f7g7h7i7j7n7s8d7l7k8e7x7m7o8f8g7p9e9f7t7G7H8D8E8F8l578G7v7u7B8m9G7A7w7y9H9I9J9K7z8j7C9z9A9B9C8i9D7F8k7I7J7K7L7N7O8h7D8H968n8o978p8q7M988r8s8t998u8v8w8x8y8z8A8B8K7P8C8L8M8N8O8I8P8Q7Q7R7E7S7U7V8J8R8S8T8U9a9T9U9V9W8V8W9b8X8Y9g9h9i8Z909c9j9k9l9m9n919d929o9p9q9r939E7T9L9F9s9t9Y9u9v9M9N839O7W949w9P9Q959R7X7Y9Saj9X7Zak9Z80a0a1a2a39xa481a59ya6a7a8a9aa82abacadaeafalag8485am8687ah8889aiaoanap8aaqar8bas8c"
-)
-
-
-def arrange(tasks):
-    d = "0123456789abcdefghijklmnopqrstuvwxyzABCDEFGHIJKLMNOPQRSTUVWXYZ"
-    seq = [62 * d.index(ORDER[i]) + d.index(ORDER[i + 1]) for i in range(0, len(ORDER), 2)]
-    assert sorted(seq) == list(range(len(tasks)))
-    return seq
+START = ("jge; zs; mask; cm; eye5; eye; ones; neye; mask0; own X; tri; heye; l1; cpb X; og a X; og b X; pos D0; pos D1; first; sel; crep- A1; "
+         "crep- A2; sum1 D1; sum0 D0; hop1; u 1 D1; u 2 D1; u 3 D1; hop2; cp1; k0; amp; pm0; x0 all D0; x1; x2; last a; low12 a; half A1; "
+         "offs B1; hc F; order A1 S0; wsel; en; fin A1 S0; ")
+STEPS = ("0:hop3; 0:cp2; 0:last b; 0:lists; 0:low12 b; gs B1; gv A1 0; 0:offs B2; 1:ch; 1:fin b D2; gv A1 1; 0:half A2; scan A1; scan B1; 0:thc; "
+         "gs B2; scan B2; 0:order A2 S0; 0:fin A2 S0; 0:l23; sub B1 0 D0; open c; sub B1 1 D1; sum A1; 0:kst; step B1 0 D0; sbit A1 0; "
+         "step B1 1 D1; sub B1 2 D0; sum B end; thr b FT; rep B2 D2; thr a F; high c; step B1 2 D0; sbit A1 1; gv A2 0; sub B1 3 D1; "
+         "add B1 0 F; add A1 0 F; add B1 2 F; step B1 3 D1; add B1 1 F; add A1 1 F; add B1 3 F end; low c; cmp B2 0 D2; gv A2 1; cmp B2 2 D2; "
+         "send c a; sbit A2 0; add B2 0 FT; add B2 2 FT; add A2 0 FT; scan A2; cmp B2 1 D2; cmp B2 3 D2; sbit A2 1; pass a F; open A2; "
+         "sum A2 end; run a; high A2; 1:fw; add B2 1 FT; add B2 3 FT; add A2 1 FT end; low A2; s16; grow a; crep A1 0; send A2 b; crep A1 1; "
+         "wrap; crep A2; pass b FT; base a S0; run b; base b D2; put a y S0; 1:fm; grow b; t1 a; t2 a; t3 a; put a t3 S0; put a t1 S0; "
+         "put a t2 S0 end; t3 b; fin a S0; t1 b; t2 b; move b D2 ")
+LAST = ("gv A1 0; fin b D2; gv A1 1; gs B1; gs B2; scan A1; gv A2 1; scan B1; scan B2; gv A2 0; open c; gaps a CM; sub B1 0 D0; rep B2 D2; "
+        "sub B1 1 D1; gaps b S0; step B1 0 D0; step B1 1 D1; sum A1; thr b FT; sub B1 2 D0; thr a F; sub B1 3 D1; cmp B2 0 D2; sbit A1 0; "
+        "step B1 2 D0; add B1 0 F; add A1 0 F; add B1 2 F; sum B end; sbit A1 1; add B1 1 F; add A1 1 F; cmp B2 2 D2; cmp B2 1 D2; cmp B2 3 D2; "
+        "scan A2; sbit A2 0; add B2 0 FT; add B2 2 FT; add A2 0 FT; step B1 3 D1; add B1 3 F end; sbit A2 1; add B2 1 FT; high c; pass a F; "
+        "add B2 3 FT; add A2 1 FT end; gap a CM; low c; send c a; out a CM; pass b FT; gap b S0; open A2; sum A2 end; high A2; out b S0; "
+        "low A2; send A2 b ")
+ON_VECTOR = (0,)
+START = ("jge; zs; mask; ones; mask0; k0; eye5; heye; en; own X; tri; l1; eye; cpb X; og a X; og b X; amp; pm0; neye; pos D1; pos D0; sum1 D1; "
+         "sum0 D0; hop1; u 1 D1; u 2 D1; u 3 D1; hop2; first; sel; crep- A1; cm; wsel; x0 all D0; x1; x2; last a; low12 a; half A1; offs B1; "
+         "hop3; hc F; order A1 S0; lists; back A1 S0; ")
+STEPS = ("1:ch; 0:last b; 0:low12 b; gv A1 1; 1:fin b D2; 0:offs b; gs B1; gs B2; rep B2 D2; open a; sub B1 0 D0; sub B1 3 CM; sub B1 1 D1; "
+         "sub B1 2 S0; step B1 0 D0; gs A2; gv A1 0; bit A1 1; 0:l23; 0:thc; scan A1; bit A1 0; scan B1; cmp B2 0 D2; cmp B2 1 D2; cmp B2 2 D2; "
+         "scan B2; thr a F; thr b FT; add A1 1 F; sub B2 3 D0; add B1 0 F; sum A1; sum B1 end; add A1 0 F; add B2 0 FT; rep A2 D2; add B2 2 FT; "
+         "add B2 1 FT; high a; low a; step B1 1 D1; step B1 2 S0; step B2 3 D0; step B1 3 CM; add B1 1 F; open b; sum B2; cmp A2 0 D2; "
+         "add A2 0 FT; add B1 2 F; add B2 3 FT; scan A2; cmp A2 1 D2; cmp A2 2 D2; cmp A2 3 D2; sum A2 end; add B1 3 F end; add A2 1 FT; high b; "
+         "pass a F; 1:fw; add A2 2 FT; run a; add A2 3 FT end; low b; s16; grow a; pass b FT; run b; 1:fm; 0:kst; grow b; t3 a; send a a; "
+         "crep A1 0; send b b; crep A1 1; wrap; t1 a; t2 a; t1 b; st3 b; t2 b; base a S0; base b D2; put a y S0; put a t1 S0; put a t3 S0; "
+         "put a t2 S0 end; fin a S0; move b D2 ")
+LAST = ("gs B1; gv A1 1; fin b D2; gv A1 0; gaps b S0; gaps a CM; bit A1 1; rep B2 D2; open a; bit A1 0; sub B1 1 D1; sub B1 0 D0; thr a F; "
+        "thr b FT; add A1 0 F; add A1 1 F; gs B2; scan A1; step B1 1 D1; step B1 0 D0; scan B1; cmp B2 0 D2; cmp B2 1 D2; cmp B2 2 D2; scan B2; "
+        "gs A2; add B1 1 F; sub B1 3 D1; sum A1; sub B1 2 D0; add B2 0 FT; add B2 1 FT; add B1 0 F; rep A2 D2; add B2 2 FT; sum B1 end; "
+        "step B1 2 D0; cmp A2 0 D2; high a; step B1 3 D1; cmp A2 1 D2; low a; scan A2; cmp A2 2 D2; cmp A2 3 D2; add B1 2 F; sub B2 3 D0; "
+        "step B2 3 D0; add A2 0 FT; add B1 3 F end; open b; sum B2; add A2 1 FT; sum A2 end; add B2 3 FT; add A2 2 FT; add A2 3 FT end; "
+        "pass a F; high b; gap a CM; low b; send a a; send b b; out a CM; pass b FT; gap b S0; out b S0 ")
+START = ("zs; jge; mask; eye5; en; k0; neye; ones; own X; heye; tri; l1; cm; cpb X; og a X; og b X; eye; pm0; mask0; wsel; first; sel; crep- A1; "
+         "wide; pos D0; pos D1; sum1 D1; sum0 D0; hop1; u 1 D1; u 2 D1; hop2; u 3 D1; hop3; x0 all D0; x1; x2; last a; low12 a; half A1; offs B1; "
+         "amp; hc F; lists; order A1 S0; back A1 S0; ")
+STEPS = ("gs B1; 0:last b; 0:l23; 0:low12 b; gv A1 0; 0:offs b; 1:fin b D2; open a; rep B2 D2; sub B1 2 S0; sub B1 1 D1; sub B1 0 D0; "
+         "sub B1 3 CM; gv A1 1; scan B1; scan A1; sum a end; gs B2; step B1 0 D0; high a; 0:thc; bit A1; cmp B2 0 D2; low a; sub B2 3 D0; "
+         "cmp B2 1 D2; cnt A1 FT; vft A1 FT; thr c F; open b; cmp B2 2 D2; scan B2; gs A2; scan A2; step B1 1 D1; step B1 2 S0; step B2 3 D0; "
+         "step B1 3 CM; spread A1 F more; add B2 0 F; add B2 1 F; add B1 0 F; rep A2 D2; add B2 2 F; add B1 1 F; thr A2 D1; add B1 2 F; "
+         "sum b end; add B2 3 F; add B1 3 F end; high b; 1:fw; pass c F; cmp A2 0 D2; cmp A2 1 D2; cmp A2 2 D2; low b; cmp A2 3 D2; send a a; "
+         "crep A1 1; send b b; wrap; crep A1 0; add A2 1 D1; add A2 0 D1; add A2 2 D1; run c; s16; grow c; add A2 3 D1 end; pass A2 D1; run A2; "
+         "0:kst; 1:fm; grow A2; 1:ch; t3 a; t3 b; base a S0; put a y S0; t1 a; t2 a; put a t1 S0; put a t3 S0; put a t2 S0 end; base b D2; t2 b; "
+         "t1 b; fin a S0; move b D2 ")
+LAST = ("gs B1; gv A1 0; fin b D2; gv A1 1; gs B2; bit A1; gaps c CM; rep B2 D2; thr c F; sub B1 1 D1; open a; sub B1 0 D0; gaps A2 S0; "
+        "cnt A1 FT; step B1 0 D0; sub B1 2 D0; scan B1; vft A1 FT; cmp B2 0 D2; scan A1; cmp B2 1 D2; cmp B2 2 D2; scan B2; step B1 1 D1; "
+        "spread A1 F more; sub B1 3 D1; add B2 0 F; add B1 1 F; sum a end; add B1 0 F; add B2 1 F; gs A2; step B1 2 D0; add B2 2 F; rep A2 D2; "
+        "sub B2 3 D0; step B1 3 D1; high a; step B2 3 D0; cmp A2 0 D2; low a; cmp A2 1 D2; cmp A2 2 D2; scan A2; cmp A2 3 D2; add B1 2 F; "
+        "thr A2 D1; add A2 0 D1; add B2 3 F; add B1 3 F end; pass c F; open b; add A2 1 D1; add A2 2 D1; gap c CM; sum b end; add A2 3 D1 end; "
+        "high b; pass A2 D1; gap A2 S0; send a a; out c CM; low b; send b b; out A2 S0 ")
+START = ("jge; zs; cm; mask; k0; heye; eye5; ones; own X; pm0; eye; tri; l1; cpb X; og a X; og b X; amp; mask0; neye; first; sel; crep- A1; "
+         "pos D0; pos D1; sum1 D1; sum0 D0; hop1; u 1 D1; u 2 D1; u 3 D1; hop2; hop3; x0 all D0; x1; x2; last a; last b; low12 a; low12 b; "
+         "half A1; offs B1; order A1 S0; hc F; offs b; back A1 S0; ")
+STEPS = ("gs B1; 0:wsel; gv A1 0; 1:fin b D2; gv A1 1; scan B1; scan A1; 0:thc; 0:en; bit A1; 0:lists; open a; rep B2 D2; sub B1 1 D1; "
+         "sub B1 2 S0; sub B1 3 CM; sub B1 0 D0; sum A1; sum B1 end; gs B2; step B1 0 D0; high a; gs A2; step B1 1 D1; step B1 2 S0; cmp B2 0 D2; "
+         "low a; cmp B2 1 D2; cmp B2 2 D2; scan B2; thr c F; add B1 0 F; sub B2 3 D0; add A1 1 F; add A1 0 F; add B2 0 F; add B2 1 F; add B2 2 F; "
+         "open b; rep A2 D2; add B1 1 F; add B1 2 F; scan A2; sum b end; cmp A2 0 D2; step B2 3 D0; add B2 3 F; step B1 3 CM; add B1 3 F end; "
+         "thr A2 D1; high b; 1:fw; pass c F; cmp A2 1 D2; cmp A2 2 D2; low b; send a a; crep A1 1; send b b; wrap; crep A1 0; add A2 1 D1; "
+         "add A2 2 D1; run c; add A2 0 D1; cmp A2 3 D2; grow c; 1:ch; s16; 0:kst; add A2 3 D1 end; pass A2 D1; run A2; grow A2; 0:l23; 1:fm; "
+         "t3 a; t3 b; t1 a; t2 a; base B1 D0; put B1 y D0; base A1 S0; put A1 y S0; put B1 t1 D0; put A1 t1 S0; put B1 t3 D0; put A1 t3 S0; "
+         "put B1 t2 D0 end; put A1 t2 S0 end; base b D2; t2 b; t1 b; fin B1 D0; fin A1 S0; move b D2 ")
+LAST = ("gs B1; gv A1 0; fin b D2; gv A1 1; gs B2; bit A1; gaps A2 S0; gaps c CM; thr c F; sub B1 1 D1; open a; rep B2 D2; sub B1 0 D0; "
+        "step B1 0 D0; step B1 1 D1; scan A1; cmp B2 0 D2; cmp B2 1 D2; cmp B2 2 D2; scan B1; scan B2; add A1 1 F; add A1 0 F; sub B1 2 D0; "
+        "sub B1 3 D1; add B1 1 F; add B2 0 F; rep A2 D2; add B1 0 F; sum A1; add B2 1 F; sum B1 end; add B2 2 F; gs A2; step B1 2 D0; "
+        "sub B2 3 D0; high a; step B1 3 D1; cmp A2 0 D2; add B1 2 F; low a; cmp A2 1 D2; thr A2 D1; add A2 0 D1; open b; scan A2; step B2 3 D0; "
+        "add B2 3 F; add B1 3 F end; add A2 1 D1; cmp A2 2 D2; cmp A2 3 D2; pass c F; sum b end; gap c CM; add A2 2 D1; add A2 3 D1 end; high b; "
+        "pass A2 D1; gap A2 S0; send a a; low b; send b b; out c CM; out A2 S0 ")
+START = ("mask; mask0; ones; heye; cm; own X; zs; jge; tri; neye; cpb X; eye5; l1; og a X; og b X; k0; amp; eye; pm0; first; sel; crep- A1; "
+         "pos D0; pos D1; sum1 D1; sum0 D0; x0 all D0; hop1; u 1 D1; u 2 D1; u 3 D1; hop2; hop3; x1; x2; last a; last b; low12 a; low12 b; "
+         "half A1; offs B1; offs b; order A1 S0; hc F; back A1 S0; ")
+STEPS = ("gs B1; 0:en; 0:wsel; gv A1 0; 1:fin b D2; gv A1 1; open a; rep B2 D2; 0:lists; scan B1; scan A1; 0:thc; bit A1; gs B2; cmp B2 0 D2; "
+         "sub B1 1 D1; sub B1 2 S0; sub B1 0 D0; sub B1 3 CM; sum A1; sum B1 end; step B1 1 D1; thr c F; thr A2 D1; add B1 1 F; high a; gs A2; "
+         "step B1 2 S0; step B1 0 D0; step B1 3 CM; low a; cmp B2 1 D2; add A1 1 F; open b; add A1 0 F; cmp B2 2 D2; cmp B2 3 D2; scan B2; 0:l23; "
+         "add B2 2 F; rep A2 D2; add B2 3 F; add B2 0 F; add B2 1 F; add B1 2 F; add B1 0 F; scan A2; cmp A2 0 D2; cmp A2 1 D2; sum b end; "
+         "add B1 3 F end; add A2 1 D1; add A2 0 D1; high b; pass c F; 1:fw; cmp A2 2 D2; low b; cmp A2 3 D2; s16; 0:kst; run c; add A2 2 D1; "
+         "add A2 3 D1 end; grow c; pass A2 D1; base A1 S0; run A2; send a a; crep A1 1; send b b; wrap; crep A1 0; put A1 y S0; base B1 D0; "
+         "put B1 y D0; base b D2; 1:fm; grow A2; t1 a; 1:ch; t3 a; t3 b; t2 a; put A1 t1 S0; put B1 t3 D0; put B1 t1 D0; put B1 t2 D0 end; "
+         "put A1 t3 S0; t1 b; t2 b; put A1 t2 S0 end; fin B1 D0; fin A1 S0; move b D2 ")
+LAST = ("gs B1; gv A1 0; fin b D2; gv A1 1; gs B2; bit A1; gaps c CM; thr c F; open a; gaps A2 S0; sub B1 0 D0; rep B2 D2; scan A1; cmp B2 0 D2; "
+        "cmp B2 1 D2; cmp B2 2 D2; sub B1 1 D1; add A1 1 F; add A1 0 F; step B1 0 D0; step B1 1 D1; gs A2; cmp B2 3 D2; scan B1; scan B2; "
+        "sum A1; sub B1 2 D0; sub B1 3 D1; add B2 1 F; add B2 2 F; rep A2 D2; add B1 0 F; sum B1 end; add B2 3 F; add B1 1 F; add B2 0 F; "
+        "step B1 3 D1; thr A2 D1; cmp A2 0 D2; cmp A2 1 D2; high a; step B1 2 D0; low a; add A2 0 D1; add A2 1 D1; add B1 2 F; add B1 3 F end; "
+        "open b; scan A2; sum b end; cmp A2 2 D2; pass c F; high b; gap c CM; add A2 2 D1; cmp A2 3 D2; low b; add A2 3 D1 end; pass A2 D1; "
+        "gap A2 S0; send a a; send b b; out c CM; out A2 S0 ")
+START = ("zs; jge; cm; mask; heye; k0; neye; ones; own X; cpb X; tri; l1; pm0; eye5; og a X; og b X; mask0; eye; first; sel; crep- A1; pos D0; "
+         "pos D1; sum1 D1; sum0 D0; hop1; u 1 D1; u 2 D1; u 3 D1; hop2; samp; hop3; x0 all D0; x1; x2; last a; last b; low12 a; low12 b; half A1; "
+         "order A1 S0; hc F; offs B1; offs b; back A1 S0; ")
+STEPS = ("0:en; 0:wsel; gv A1 0; 1:fin b D2; gv A1 1; 0:fw; gs B1; scan B1; open a; 1:val- all FT; 0:lists; rep B2 D2; sub B1 1 D1; sub B1 3 CM; "
+         "sub B1 0 D0; sub B1 2 S0; gs B2; scan A1; 0:thc; bit A1; cmp B2 0 D2; sum A1; sum B1 end; step B1 1 D1; high a; gs A2; step B1 2 S0; "
+         "step B1 0 D0; low a; cmp B2 1 D2; cmp B2 2 D2; cmp B2 3 D2; scan B2; 0:kst; scan A2; thr c F; add B1 1 F; thr A2 D1; add A1 0 F; "
+         "add A1 1 F; add B2 1 F; open b; add B2 2 F; rep A2 D2; add B2 0 F; add B2 3 F; add B1 2 F; cmp A2 0 D2; cmp A2 1 D2; cmp A2 2 D2; "
+         "add B1 0 F; sum b end; step B1 3 CM; high b; add B1 3 F end; add A2 0 D1; pass c F; 1:inc- all FT; add A2 1 D1; run c; add A2 2 D1; "
+         "low b; cmp A2 3 D2; s16; grow c; add A2 3 D1 end; pass A2 D1; send a a; crep A1 0; crep A1 1; send b b; wrap; base A1 S0; run A2; "
+         "base B1 D0; base b D2; put B1 y D0; put A1 y S0; 0:l23; grow A2; 0:fm; t3 a; t1 a; put A1 t1 S0; put B1 t1 D0; put B1 t3 D0; t2 a; "
+         "put B1 t2 D0 end; put A1 t3 S0; put A1 t2 S0 end; t3 b; fin B1 D0; 1:ch; fin A1 S0; t2 b; t1 b; move b D2 ")
+LAST = ("gs B1; gv A1 1; fin b D2; gv A1 0; gs B2; thr c F; open a; val- all FT; rep B2 D2; sub B1 3 CM; sub B1 0 D0; sub B1 2 S0; sub B1 1 D1; "
+        "bit A1; scan B1; cmp B2 0 D2; cmp B2 1 D2; cmp B2 2 D2; cmp B2 3 D2; step B1 0 D0; step B1 2 S0; step B1 1 D1; step B1 3 CM; gs A2; "
+        "inc- all FT; scan A1; scan B2; add A1 1 F; add B1 0 F; add A1 0 F; add B1 2 F; add B1 1 F; thr A2 D1; add B2 1 F; add B2 2 F; "
+        "add B2 0 F; add B2 3 F; rep A2 D2; sum A1; sum B1 end; add B1 3 F end; incs c CM; cmp A2 0 D2; high a; pass c F; cmp A2 1 D2; low a; "
+        "scan A2; add A2 0 D1; add A2 1 D1; gap c CM; open b; sum b end; cmp A2 2 D2; add A2 2 D1; high b; send a a; cmp A2 3 D2; out c CM; "
+        "low b; send b b; add A2 3 D1 end; incs A2 S0; pass A2 D1; gap A2 S0; out A2 S0 ")
+ROUNDS = [START + STEPS, STEPS, LAST]
+NATURAL = False
 
 
 def rank_program(g, core, T, topo):
@@ -73,360 +149,22 @@ def rank_program(g, core, T, topo):
     n_ranks = len(T.cores)
     own = V * rank
     queue = {"v": g.vector, "s": g.scalar, "p": g.tensor, "g": g, "y": g.sync}
-    tasks = []
     touches = {}
+    known = {q: {} for q in queue}
+    total = {}
 
     def A(name, lo, hi, step=1, parts=None):
         t = T[name]
         if parts is not None:
-            ap = t[0:parts, lo:hi]
+            ap = t[0:parts, lo:hi:step] if step > 1 else t[0:parts, lo:hi]
         elif step > 1:
             ap = t[:, lo:hi:step]
         else:
             ap = t[:, lo:hi]
-        return ap, (name, lo, hi, len(range(lo, hi, step)))
+        return ap, (name, lo, hi, step)
 
-    def task(q, call, reads, writes, cost, sem=None, count=0, lat=0.0, dma=0.0, also=()):
-        deps = set(also)
-        for rs, w in ((reads, False), (writes, True)):
-            for r in rs:
-                for lo2, hi2, w2, q2, j in touches.get(r[0], []):
-                    if (q2 != q or q == "p") if r[0] in PSUM else ((w or w2) and r[1] < hi2 and lo2 < r[2]):
-                        deps.add(j)
-        for rs, w in ((reads, False), (writes, True)):
-            for r in rs:
-                old = touches.get(r[0], [])
-                if r[0] in PSUM:
-                    old = [] if q == "p" else old
-                elif w and len(r) > 3 and r[3] == r[2] - r[1]:
-                    old = [x for x in old if not (r[1] <= x[0] and x[1] <= r[2])]
-                touches[r[0]] = old + [(r[1], r[2], w, q, len(tasks))]
-        kind = "g" if any(SCRATCH[r[0]][2] == "uint16" for r in reads) and writes[0][0] != "s16" else "p" if q == "p" else "e" if q in "vs" and not dma else "o"
-        tasks.append({"q": q, "call": call, "deps": sorted(deps), "cost": cost, "sem": sem, "count": count, "lat": lat, "dma": dma,
-                      "kind": kind})
-        return len(tasks) - 1
-
-    def ind(win, off):
-        return win[0].indirect(off[0]), win[1], off[1]
-
-    def regs(*xs):
-        return [r for x in xs if isinstance(x, tuple) for r in x[1:]]
-
-    def val(x):
-        return x[0] if isinstance(x, tuple) else x
-
-    def narrow(*xs):
-        return 0.5 if all(SCRATCH[x[1][0]][2] in ("bfloat16", "float16", "uint16") for x in xs) else 1.0
-
-    def price(out, a, k):
-        n = out[1][3]
-        return 60.0 + n * OPT["g"] if len(a) == 3 else 50.0 + max(64.0, n * k) * OPT["e"]
-
-    def ts(out, a, s1, s2, op0, op1=None):
-        if op1 is None:
-            call = lambda: g.vector.tensor_scalar(out[0], a[0], val(s1), None, op0)
-        else:
-            call = lambda: g.vector.tensor_scalar(out[0], a[0], val(s1), val(s2), op0, op1)
-        task("v", call, regs(a, s1, s2), regs(out), price(out, a, narrow(out, a)))
-
-    def tt(out, a, b, o):
-        k = (1.0 if a[1][0] in PSUM or b[1][0] in PSUM else 2.0) * (OPT["tt2"] if narrow(out, a, b) < 1 else 1.0)
-        task("v", lambda: g.vector.tensor_tensor(out[0], a[0], b[0], o), regs(a, b), regs(out), price(out, a, k))
-
-    def cp(out, a):
-        task("v", lambda: g.vector.tensor_copy(out[0], a[0]), regs(a), regs(out), price(out, a, narrow(out, a)))
-
-    def fill(out, c):
-        task("v", lambda: g.vector.memset(out[0], c), [], regs(out), price(out, out, narrow(out)))
-
-    def act(out, a, func, bias=0.0, scale=1.0, more=0.0):
-        task("s", lambda: g.scalar.activation(out[0], a[0], func, bias=bias, scale=scale), regs(a), regs(out), more + price(out, a, 1.0))
-
-    def step(out, a):
-        act(out, a, ACT.Sigmoid, bias=-128.0, scale=256.0)
-
-    def mm(out, lhs, rhs, start, stop):
-        k = 4.0 if SCRATCH[rhs[1][0]][2] == "float32" else 1.0
-        task("p", lambda: g.tensor.matmul(out[0], lhs[0], rhs[0], start, stop), regs(lhs, rhs), regs(out),
-             20.0 + max(64, out[1][3]) * k * OPT["pe"])
-
-    def iota(out, pattern, base, mult):
-        task("g", lambda: g.iota(out[0], pattern, base, mult, allow_small_or_imprecise_dtypes=True), [], regs(out),
-             130.0 + 2 * out[1][3] * OPT["e"])
-
-    def load(q, out, src, sem, busy, also=()):
-        return task(q, lambda: queue[q].dma_start(out[0], src), [], regs(out), 100.0, sem, 16, 1700.0 + busy, busy, also)
-
-    def store(dst, a, busy):
-        task("y", lambda: g.sync.dma_start(dst, a[0]), regs(a), [], 100.0, "st", 16, 1700.0 + busy, busy)
-
-    others = [T.cores[(rank + d) % n_ranks] for d in range(1, n_ranks)]
-    mask = topo.mask(core, others[0])
-    for o in others:
-        mask &= topo.mask(core, o)
-    n_eng = bin(mask).count("1")
-    ids = [DstId(rid=topo.addr(o)[0], pnc=topo.addr(o)[1]) for o in others]
-
-    def share(table, lo, hi, arr, loc, more=0.0):
-        src = A(table, own + lo, own + hi)
-        busy = 56 * (35.0 + (hi - lo) / 10.0)
-
-        def call():
-            g.remote_dma_fused([RemoteDMATransfer(dst_ids=ids, dma_engine_mask=mask, remote_sem=T.sem[arr], srcs=[src[0]],
-                                                  dsts=[src[0] for o in others])], local_sem=T.sem[loc])
-        i = task("g", call, regs(src), [], 600.0, loc, n_eng, 1200.0 + more + busy, busy)
-        landed = [(table, V * r + lo, V * r + hi) for r in range(n_ranks) if r != rank]
-        task("far", None, [], landed, 200.0, arr, n_eng * (n_ranks - 1), also=[i])
-        return i
-
-    EYE, NEYE, HEYE, EYE16 = A("eye", 0, 128), A("neye", 0, 128), A("heye", 0, 128), A("eye16", 0, 128)
-    TRI, BD = A("tri", 0, 128), A("bd", 0, 128)
-    L1 = A("l1", 0, 32)
-
-    def full(name):
-        return A(name, 0, V)
-
-    i = load("y", A("T0", own, own + V), T.c0[:], "ldc", 700.0)
-    load("s", full("cpi"), T.cp[:], "ldp", 1100.0)
-    for q, out, src, sem, busy in (("y", full("gpi"), T.gp[:], "ldg", 1100.0), ("s", A("rfi", 0, 32), T.rf[:], "ldr", 330.0),
-                                   ("y", full("thi"), T.th[:], "ldt", 1100.0)):
-        j = load(q, out, src, sem, busy)
-        tasks[j]["behind"] = j - 2
-    iota(A("J", 0, 144), [[1, 144]], 0, -1)
-    iota(A("K", 0, 128), [[16, 8], [0, 16]], 0, -1)
-    iota(full("pos2"), [[2, V]], 0, 0)
-    i = share("T0", 0, V, "arr0", "sent", 1500.0)
-    iota(A("RM", 0, 16 * CH), [[0, 4 * CH], [256, 4]], 0, 0)
-    tasks[-1]["behind"] = i
-
-    JS = A("J", 0, 128)
-    fill(A("half", 0, 128, parts=1), 0.5)
-    fill(A("c192", 0, 128, parts=1), 192.0)
-    fill(A("c256", 0, 256, parts=1), 256.0)
-    fill(A("zero", 0, 128, parts=1), 0.0)
-    fill(A("en", 0, 144), 0.0)
-    ts(HEYE, JS, 0.0, -HUGE, ALU.is_equal, ALU.mult)
-    ts(A("jge", 0, 128), JS, 0.0, None, ALU.is_ge)
-    fill(A("en", 15, 144, 16), -1.0)
-    ts(EYE, JS, 0.0, None, ALU.is_equal)
-    ts(NEYE, JS, 0.0, -1.0, ALU.is_equal, ALU.mult)
-    ts(EYE16, JS, 0.0, None, ALU.is_equal)
-    ts(A("j1", 0, 128), JS, 1.0, None, ALU.is_equal)
-    ts(A("k0", 0, 128), A("K", 0, 128), 0.0, None, ALU.is_equal)
-    act(A("zs", 0, 128), A("K", 0, 128), ACT.Sigmoid, bias=128.0, scale=-256.0, more=1300.0)
-    task("v", lambda: g.vector.tensor_reduce(T.pm0[:, 0:1], T.k0[:, 0:128], AxisListType.X, ALU.max), [("k0", 0, 128)], [("pm0", 0, 1)], 190.0)
-    cp(L1, A("rfi", 0, 32))
-    ts(A("l1a", 0, 32), A("rfi", 0, 32), 2.0, 1.0, ALU.mult, ALU.add)
-    ts(A("wsel", 0, 144), A("J", 0, 144), 15.0, A("pm0", 0, 1), ALU.is_equal, ALU.mult)
-    tt(A("tri16", 0, 128), A("jge", 0, 128), A("zs", 0, 128), ALU.mult)
-    tt(TRI, A("jge", 0, 128), A("zs", 0, 128), ALU.mult)
-    tt(A("j1", 0, 128), A("j1", 0, 128), A("zs", 0, 128), ALU.mult)
-    tt(BD, EYE, A("j1", 0, 128), ALU.subtract)
-    for bank in ("D0", "D1"):
-        mm(full(bank), A("half", 0, 128, parts=1), A("pos2", 0, V, parts=1), True, False)
-    act(full("r1"), ind(full("pos2"), L1), ACT.Copy)
-    ts(full("ownb"), full("cpi"), -1.0, 1.0, ALU.mult, ALU.add)
-    act(full("cpb"), full("ownb"), ACT.Identity, bias=1.0, scale=-1.0)
-    tt(full("og"), full("gpi"), full("ownb"), ALU.mult)
-    act(A("r23", 0, V), ind(full("r1"), L1), ACT.Copy)
-    mm(full("D1"), HEYE, full("cpb"), False, False)
-    mm(full("D1"), A("tri16", 0, 128), full("og"), False, True)
-    mm(full("D0"), A("tri16", 0, 128), full("og"), False, True)
-    act(full("u1"), full("D1"), ACT.Relu, bias=float(own + BIG))
-    ts(full("x0"), full("D0"), float(own), None, ALU.add)
-    act(full("u2"), full("D1"), ACT.Relu, bias=float(own + 2 * BIG))
-    act(full("u3"), full("D1"), ACT.Relu, bias=float(own + 3 * BIG))
-    act(A("r23", V, 2 * V), ind(A("r23", 0, V), L1), ACT.Copy)
-    tt(full("x1"), ind(full("x0"), L1), full("u1"), ALU.max)
-    tt(full("x2"), ind(full("x1"), L1), full("u2"), ALU.max)
-    R0 = OPT["r0"]
-    for lo, hi in zip(R0[:-1], R0[1:]):
-        tt(A("x3", lo, hi), ind(full("x2"), A("l1", lo // 16, hi // 16)), A("u3", lo, hi), ALU.max)
-        ts(A("x3", lo, hi), A("x3", lo, hi), 4095, None, ALU.bitwise_and)
-        cp(A("soff", lo, hi), A("x3", lo, hi))
-    for q in range(16):
-        mm(A("CM", 0, 64), A("wsel", 15 - q, 143 - q), A("r23", q, 2 * V, 16), q == 0, q == 15)
-    ts(A("l23", 0, 32), A("CM", 0, 32), 1.0, None, ALU.add)
-    ts(A("l23", 32, 64), A("CM", 32, 64), 0.0, None, ALU.add)
-    cp(full("thb"), full("thi"))
-    ts(A("eyeh", 0, 128), JS, 0.0, 0.5, ALU.is_equal, ALU.mult)
-    act(full("cp1"), ind(full("cpb"), L1), ACT.Copy, scale=0.5)
-    act(full("cp2"), ind(full("cp1"), L1), ACT.Copy, scale=0.5)
-    for j, name in enumerate(("cpb", "cp1", "cp2")):
-        mm(full("F1"), EYE, full(name), j == 0, j == 2)
-    act(full("kst"), full("F1"), ACT.Identity, bias=1.0 / 32, scale=0.25)
-
-    def mine(r, lo, hi):
-        return A("T%d" % r, own + lo, own + hi)
-
-    def gather(r, lo, hi, on_v):
-        src = ind(A("T%d" % r, 0, 4096 + (2 if r else 0)), A("soff", lo, hi))
-        if on_v:
-            cp(gathered(lo, hi), src)
-        else:
-            act(gathered(lo, hi), src, ACT.Copy)
-
-    def sets(c):
-        return (c[1] - c[0]) // 32
-
-    def scan(c):
-        p, m, rm = gathered(*c), A("M", 16 * c[0], 16 * c[1]), A("RM", 0, 16 * (c[1] - c[0]))
-        task("v", lambda: g.vector.tensor_tensor_scan(m[0], rm[0], p[0], 0.0, ALU.min, ALU.max), regs(p, rm), regs(m), price(m, p, 0.5))
-
-    def crep(r, c, bank):
-        rep = 16 // sets(c)
-        for j in range(rep):
-            mm(A(bank, j, 512, rep), EYE, mine(r, *c), True, True)
-
-    def gathered(lo, hi):
-        return A("P", 16 * lo, 16 * hi)
-
-    def links(c, s):
-        return A("P", 16 * c[0] + s, 16 * c[1], sets(c))
-
-    def bits(c, s):
-        return A("B", 16 * c[0] + 512 * s, 16 * c[0] + 512 * (s + 1))
-
-    def compare(c, s, bank):
-        tt(bits(c, s), links(c, s), full(bank), ALU.is_gt)
-
-    def compare_s(r, c, s, bank, early):
-        rep = 16 // sets(c)
-        if early:
-            mm(full(bank), A("zero", 0, 128, parts=1), A("ownb", 0, V, parts=1), True, False)
-        else:
-            mm(full(bank), EYE, links(c, s), True, False)
-        for j in range(rep):
-            mm(A(bank, j, 512, rep), NEYE, mine(r, *c), False, j == rep - 1 and not early)
-        if early:
-            mm(full(bank), EYE, links(c, s), False, True)
-        step(bits(c, s), full(bank))
-
-    def count(r, c, bank, ss):
-        rep = 16 // sets(c)
-        f = A(bank, *c)
-        late = False
-        mm(f, HEYE, A("cpb", *c), True, False)
-        if not late:
-            mm(f, EYE, A("thb", *c), False, False)
-        for s in ss:
-            for j in range(rep):
-                k = sets(c) * j + s
-                lo = 16 * c[0] + 512 * s
-                mm(f, A("en", 15 - k, 143 - k), A("B", lo + j, lo + 512, rep), False, s == ss[-1] and j == rep - 1 and not late)
-        if late:
-            mm(f, EYE, A("thb", *c), False, True)
-
-    def sums(r, c):
-        x = A("X", *c)
-        mm(x, A("c192", 0, 128, parts=1), A("c256", 0, c[1] - c[0], parts=1), True, False)
-        mm(x, EYE, mine(r, *c), False, False)
-        for b in range(4):
-            mm(x, EYE, A("M", 16 * c[0] + 4 * b + 3, 16 * c[1], 16), False, b == 3)
-
-    def registers(r, lo, hi, tag):
-        if tag in OPT["rounds"][r]["high_v"]:
-            ts(A("yq", lo, hi), A("X", lo, hi), -127.5, None, ALU.add)
-        else:
-            act(A("yq", lo, hi), A("X", lo, hi), ACT.Identity, bias=-127.5)
-        tt(mine(r + 1, lo, hi) if r < 2 else A("cout", lo, hi), A("X", lo, hi), A("yq", lo, hi), ALU.subtract)
-        if r < 2:
-            return share("T%d" % (r + 1), lo, hi, "arr%d%s" % (r + 1, tag), "sent")
-        store(T.yc[:, lo:hi], A("cout", lo, hi), 500.0)
-
-    def running(r, lo, hi, bank):
-        step(A("mb", lo, hi), A(bank, lo, hi))
-        n = hi - lo
-        if r < 2:
-            mm(A("CM", 1, 2 * n, 2), HEYE, A("cpb", lo, hi), True, False)
-            mm(A("CM", 1, 2 * n, 2), TRI, A("mb", lo, hi), False, True)
-            mm(A("CM", 0, 2 * n, 2), TRI, A("mb", lo, hi), True, True)
-            step(A("W%d" % r, 2 * lo, 2 * hi), A("CM", 0, 2 * n))
-        else:
-            mm(A("CM", 0, n), TRI, A("mb", lo, hi), True, True)
-            step(A("W2", lo, hi), A("CM", 0, n))
-
-    def shift(r, lo, hi, bank, by):
-        mm(A(bank, lo, hi), EYE16, A("s16", lo, hi), True, False)
-        mm(A(bank, lo, hi), EYE, A("kst", lo, hi), False, False)
-        mm(A(bank, lo, hi), A("eyeh", 0, 128), A("W%d" % r, 2 * lo + 1, 2 * hi, 2), False, False)
-        for j, (lst, at) in enumerate((("l1a", 0), ("l23", 0), ("l23", 32))):
-            t = A("t%d" % (j + 1), lo, hi)
-            src = ind(A("W%d" % r, 0, 2 * V), A(lst, at + lo // 16, at + hi // 16))
-            if by[j] == "v":
-                ts(t, src, 0.25 / 2 ** j, None, ALU.mult)
-            else:
-                act(t, src, ACT.Copy, scale=0.25 / 2 ** j)
-            mm(A(bank, lo, hi), EYE, t, False, j == 2)
-        ts(A("soff", lo, hi), A(bank, lo, hi), ROUND, ROUND - 2048.0, ALU.add, ALU.subtract)
-
-    def gaps(lo, hi, bank):
-        mm(A(bank, lo, hi), BD, A("W0", 2 * lo, 2 * hi, 2), True, False)
-        mm(A(bank, lo, hi), BD, A("W1", 2 * lo, 2 * hi, 2), False, False)
-        mm(A(bank, lo, hi), BD, A("W2", lo, hi), False, True)
-        tt(A("gout", lo, hi), A(bank, lo, hi), A("gpi", lo, hi), ALU.add)
-        store(T.yg[:, lo:hi], A("gout", lo, hi), 280.0 + 1.6 * (hi - lo))
-
-    for r in range(3):
-        o = OPT["rounds"][r]
-        cuts = o["cuts"]
-        chunks = list(zip(cuts[:-1], cuts[1:]))
-        for lo, hi in zip(o["gathers"][:-1], o["gathers"][1:]):
-            gather(r, lo, hi, lo in o["by_v"])
-            if lo not in o["by_v"]:
-                if lo:
-                    tasks[-1]["behind"] = prev
-                prev = len(tasks) - 1
-        if r < 2:
-            ts(full("s16"), full("soff"), -2048.0, None, ALU.add)
-        sent, first, n_d, n_c = 0, None, 0, 0
-        n0 = len(tasks)
-        for c in zip(o["scans"][:-1], o["scans"][1:]):
-            scan(c)
-            sums(r, c)
-            if c[1] in o["sends"]:
-                i = registers(r, sent, c[1], "abc"[o["sends"].index(c[1])])
-                first, sent = (i if first is None else first), c[1]
-        for t in tasks[n0:]:
-            t["boost"] = o["boost"]
-        if r < 2:
-            t = "T%d" % (r + 1)
-            task("g", lambda t=t: g.affine_select(T[t][:, 4096:4098], T[t][:, 0:2], [[0, 2]], ALU.is_ge, 0.0, 0, 0),
-                 [(t, 0, 2)], [(t, 4096, 4098)], 170.0, also=[first + 1])
-            tasks[-1]["behind"] = i
-        for j in o["order"]:
-            c = chunks[j]
-            n_s = o["by_s"][j]
-            for s in range(n_s):
-                banks = o["banks"]
-                compare_s(r, c, s, banks[n_d % len(banks)], s < len(banks))
-                n_d += 1
-            if n_s < sets(c):
-                crep(r, c, "CR%d" % (n_c % 2))
-                for s in range(n_s, sets(c)):
-                    compare(c, s, "CR%d" % (n_c % 2))
-                n_c += 1
-            count(r, c, o["fbank"][j], list(range(sets(c))))
-            if j == 1:
-                running(r, 0, c[1], "F0")
-            elif j > 1:
-                running(r, c[0], c[1], o["fbank"][j])
-        if r < 2:
-            for j, (lo, hi, by) in enumerate(OPT["shifts"]):
-                shift(r, lo, hi, ["D1", "D0", "F1"][j], by)
-        else:
-            for j, (lo, hi) in enumerate(zip(o["gaps"][:-1], o["gaps"][1:])):
-                gaps(lo, hi, ["D1", "D0"][j % 2])
-
-    if "seq" not in PLAN:
-        plan = [dict(t) for t in tasks]
-        for t in plan:
-            if "behind" in t:
-                t["deps"] = sorted(set(t["deps"] + [t["behind"]]))
-        PLAN["seq"] = OPT.get("arrange", arrange)(plan)
-    known = {q: {} for q in queue}
-    total = {}
-    mark = {}
+    def meet(a, b):
+        return a[1] < b[1] and b[0] < a[2] and (a[1] - b[0]) % math.gcd(a[3], b[2]) == 0
 
     def wait(q, sem, count, seen):
         if known[q].get(sem, 0) >= count:
@@ -437,27 +175,376 @@ def rank_program(g, core, T, topo):
             if known[q].get(s, 0) < c:
                 known[q][s] = c
 
-    for i in PLAN["seq"]:
-        t = tasks[i]
-        q = t["q"]
-        if q == "far":
-            mark[i] = (t["sem"], t["count"], {})
-            continue
+    def note(q, reads, writes, mark):
+        for rs, w in ((reads, False), (writes, True)):
+            for r in rs:
+                old = touches.get(r[0], [])
+                if r[0] in PSUM:
+                    old = [] if q == "p" else old
+                elif w and r[3] == 1:
+                    old = [x for x in old if not (r[1] <= x[0] and x[1] <= r[2])]
+                touches[r[0]] = old + [(r[1], r[2], r[3], w, q, mark)]
+
+    def issue(q, call, reads, writes, sem=None, count=1, after=()):
         need = {}
-        for d in t["deps"]:
-            if q == "p" and tasks[d]["q"] == "p":
-                continue
-            sem, count, seen = mark[d]
-            if count > need.get(sem, (0, None))[0]:
-                need[sem] = (count, seen)
-        for sem in sorted(need, key=lambda s: s == COUNTER.get(q)):
-            wait(q, sem, need[sem][0], need[sem][1])
-        ins = t["call"]()
-        sem, count = (t["sem"], t["count"]) if t["sem"] else (COUNTER[q], 1)
+        marks = list(after)
+        for rs, w in ((reads, False), (writes, True)):
+            for r in rs:
+                for x in touches.get(r[0], []):
+                    if (x[4] != q or (q != "p" and (w or x[3]))) if r[0] in PSUM else ((w or x[3]) and meet(r, x)):
+                        marks.append(x[5])
+        for s, c, seen in marks:
+            if c > need.get(s, (0, None))[0]:
+                need[s] = (c, seen)
+        for s in sorted(need, key=lambda s: s == COUNTER.get(q)):
+            wait(q, s, need[s][0], need[s][1])
+        ins = call()
+        sem = sem or COUNTER[q]
         if ins is not None:
             ins.then_inc(T.sem[sem], count)
         total[sem] = total.get(sem, 0) + count
-        mark[i] = (sem, total[sem], dict(known[q]))
+        mark = (sem, total[sem], dict(known[q]))
+        note(q, reads, writes, mark)
+        return mark
+
+    def ind(win, off):
+        return win[0].indirect(off[0]), win[1], off[1]
+
+    def regs(*xs):
+        return [r for x in xs if isinstance(x, tuple) for r in x[1:]]
+
+    def val(x):
+        return x[0] if isinstance(x, tuple) else x
+
+    def ts(out, a, s1, s2, op0, op1=None):
+        if op1 is None:
+            call = lambda: g.vector.tensor_scalar(out[0], a[0], val(s1), None, op0)
+        else:
+            call = lambda: g.vector.tensor_scalar(out[0], a[0], val(s1), val(s2), op0, op1)
+        issue("v", call, regs(a, s1, s2), regs(out))
+
+    def tt(out, a, b, o):
+        issue("v", lambda: g.vector.tensor_tensor(out[0], a[0], b[0], o), regs(a, b), regs(out))
+
+    def cp(out, a):
+        issue("v", lambda: g.vector.tensor_copy(out[0], a[0]), regs(a), regs(out))
+
+    def fill(out, c):
+        issue("v", lambda: g.vector.memset(out[0], c), [], regs(out))
+
+    def act(out, a, func, bias=0.0, scale=1.0):
+        issue("s", lambda: g.scalar.activation(out[0], a[0], func, bias=bias, scale=scale), regs(a), regs(out))
+
+    def step(out, a):
+        act(out, a, ACT.Sigmoid, bias=-128.0, scale=256.0)
+
+    def mm(out, lhs, rhs, start, stop):
+        issue("p", lambda: g.tensor.matmul(out[0], lhs[0], rhs[0], start, stop), regs(lhs, rhs), regs(out))
+
+    def iota(out, pattern, base, mult):
+        issue("g", lambda: g.iota(out[0], pattern, base, mult, allow_small_or_imprecise_dtypes=True), [], regs(out))
+
+    def select(out, a, pattern, op, base, mult):
+        issue("g", lambda: g.affine_select(out[0], a[0], pattern, op, 0.0, base, mult), regs(a), regs(out))
+
+    def load(q, out, src, sem, after=()):
+        issue(q, lambda: queue[q].dma_start(out[0], src), [], regs(out), sem, 16, after)
+
+    def store(dst, a):
+        issue("y", lambda: g.sync.dma_start(dst, a[0]), regs(a), [], "st", 16)
+
+    others = [T.cores[(rank + d) % n_ranks] for d in range(1, n_ranks)]
+    mask = topo.mask(core, others[0])
+    for o in others:
+        mask &= topo.mask(core, o)
+    n_eng = bin(mask).count("1")
+    ids = [DstId(rid=topo.addr(o)[0], pnc=topo.addr(o)[1]) for o in others]
+
+    def share(table, lo, hi, arr):
+        src = A(table, own + lo, own + hi)
+
+        def call():
+            g.remote_dma_fused([RemoteDMATransfer(dst_ids=ids, dma_engine_mask=mask, remote_sem=T.sem[arr], srcs=[src[0]],
+                                                  dsts=[src[0] for o in others])], local_sem=T.sem["sent"])
+        issue("g", call, regs(src), [], "sent", n_eng)
+        mark = (arr, n_eng * (n_ranks - 1), {})
+        note("far", [], [(table, V * r + lo, V * r + hi, 1) for r in range(n_ranks) if r != rank], mark)
+        return mark
+
+    EYE, NEYE, HEYE, TRI = A("eye", 0, 128), A("neye", 0, 128), A("heye", 0, 128), A("tri", 0, 128)
+    JS, KS, L1 = A("J", 0, 128), A("K", 0, 128), A("l1", 0, 32)
+
+    def full(name):
+        return A(name, 0, V)
+
+    def mine(r, lo, hi):
+        return A("T%d" % r, own + lo, own + hi)
+
+    def row(name):
+        return A(name, 0, 128, parts=1)
+
+    def whole(bank, lo, hi, stop):
+        mm(A(bank, lo, hi), row("cm"), A("RM", 1, 4 * (hi - lo), 4, parts=1), False, False)
+        mm(A(bank, lo, hi), row("cm"), A("RM", 0, 4 * (hi - lo), 4, parts=1), False, stop)
+
+    def place(bank, name, lo, hi, start, stop):
+        a = lo
+        while a < hi:
+            b = a + 128 if a in ON_VECTOR else min([x for x in ON_VECTOR if x > a] + [hi])
+            end = stop and b == hi
+            if a in ON_VECTOR:
+                for j in range(4):
+                    h, q = j // 2, j % 2
+                    mm(A(bank, a + 64 * h, a + 64 * h + 64), A("sel", 128 * j, 128 * j + 128), A(name, a + q, b, 2),
+                       start and q == 0, (start and q == 1) or (end and j == 3))
+            else:
+                mm(A(bank, a, b), EYE, A(name, a, b), start, end)
+            a = b
+
+    def sigmoid(out, a, sign):
+        act(out, a, ACT.Sigmoid, bias=128.0, scale=256.0 * sign)
+
+    def lists():
+        for q in range(16):
+            mm(A("FT", 0, 64), A("wsel", 15 - q, 143 - q), A("r23", q, 2 * V, 16), q == 0, q == 15)
+
+    def first():
+        load("y", full("thi"), T.th[:], "ldt", [share("T0", 0, V, "arr0")])
+
+    def sel():
+        for j in range(4):
+            select(A("sel", 128 * j, 128 * j + 128), A("ones", 0, 128), [[-16, 8], [1000, 2], [-2 if NATURAL else -1, 8]], ALU.is_equal,
+                   -(1 if NATURAL else 8) * (j // 2) - 1000 * (j % 2), 1)
+
+    def wide():
+        for j in range(2):
+            select(A("spread", V * j, V * j + V), full("ones"), [[-16, 4], [0, 8], [-1, 16]], ALU.is_equal, -64 * j, 1)
+
+    def en():
+        fill(A("en", 0, 144), 0.0)
+        fill(A("en", 15, 144, 16), -1.0)
+
+    single = {
+        "mask": lambda: fill(A("RM", 0, 2048), 256.0), "mask0": lambda: fill(A("RM", 0, 2048, 4), -256.0),
+        "ones": lambda: fill(full("ones"), 1.0), "cm": lambda: fill(row("cm"), 49152.0), "zero": lambda: fill(row("zero"), 0.0), "ch": lambda: fill(row("ch"), 63.0 / 128),
+        "jge": lambda: sigmoid(A("jge", 0, 128), JS, 1), "zs": lambda: sigmoid(A("zs", 0, 128), KS, -1),
+        "heye": lambda: ts(HEYE, JS, 0.0, -HUGE, ALU.is_equal, ALU.mult), "eye": lambda: ts(EYE, JS, 0.0, None, ALU.is_equal),
+        "neye": lambda: ts(NEYE, JS, 0.0, -1.0, ALU.is_equal, ALU.mult),
+        "eye5": lambda: ts(A("eye5", 0, 128), JS, 0.0, 5.0, ALU.is_equal, ALU.mult),
+        "tri": lambda: tt(TRI, A("jge", 0, 128), A("zs", 0, 128), ALU.mult),
+        "k0": lambda: ts(A("k0", 0, 128), KS, 0.0, None, ALU.is_equal),
+        "pm0": lambda: issue("v", lambda: g.vector.tensor_reduce(T.pm0[:, 0:1], T.k0[:, 0:128], AxisListType.X, ALU.max),
+                             [("k0", 0, 128, 1)], [("pm0", 0, 1, 1)]),
+        "wsel": lambda: ts(A("wsel", 0, 144), A("J", 0, 144), 15.0, A("pm0", 0, 1), ALU.is_equal, ALU.mult),
+        "fw": lambda: act(A("fw", 0, 128), EYE, ACT.Identity, bias=-1.0 / 32, scale=3.0 / 64),
+        "fm": lambda: tt(A("fm", 0, 128), TRI, A("fw", 0, 128), ALU.mult),
+        "first": first, "sel": sel, "en": en, "lists": lists, "wide": wide,
+        "l1": lambda: cp(L1, A("rfi", 0, 32)), "l23": lambda: ts(A("l23", 0, 64), A("FT", 0, 64), 256.0, None, ALU.add),
+        "hop1": lambda: act(full("r1"), ind(full("pos"), L1), ACT.Copy),
+        "hop2": lambda: act(A("r23", 0, V), ind(full("r1"), L1), ACT.Copy),
+        "hop3": lambda: act(A("r23", V, 2 * V), ind(A("r23", 0, V), L1), ACT.Copy),
+        "cp1": lambda: act(full("cp1"), ind(full("cpb"), L1), ACT.Copy, scale=0.5),
+        "x1": lambda: tt(full("x1"), ind(full("x0"), L1), full("u1"), ALU.max),
+        "x2": lambda: tt(full("x2"), ind(full("x1"), L1), full("u2"), ALU.max),
+        "thc": lambda: tt(full("thc"), full("thi"), full("F"), ALU.add),
+        "kst": lambda: ts(full("kst"), full("x3"), -0.055 / BIG, 0.46, ALU.mult, ALU.add),
+        "amp": lambda: ts(full("amp"), full("cpb"), -63.0 / 128, 0.5, ALU.mult, ALU.add),
+        "samp": lambda: act(full("amp"), full("cpb"), ACT.Identity, bias=0.5, scale=-63.0 / 128),
+        "s16": lambda: ts(full("s16"), full("soff"), -2048.0, None, ALU.add),
+    }
+
+    def run_step(r, name, lo, hi, more):
+        n = hi - lo
+        mb = "mb%d" % r
+        table = A("T%d" % max(r, 0), 0, 4096 + (2 if r else 0))
+        fused = lo - lo % 128 in ON_VECTOR
+
+        def links(name, first=0, step=1):
+            return A(name, 16 * lo + int(first), 16 * hi, int(step))
+
+        def piece(name, s, first=0, step=1):
+            if NATURAL:
+                return links(name, s, 2 if fused else 4)
+            at, width = (1024 * int(s), 8) if fused else (2048 + 1536 * int(s) + 4 * (lo - 128), 4)
+            return A(name, at + first, at + width * n, step)
+
+        if name in single:
+            single[name]()
+        elif name == "pos":
+            mm(full(more[0]), row("ones"), A("pos", 0, V, parts=1), True, False)
+        elif name == "own":
+            ts(full(more[0]), full("cpi"), -1.0, 1.0, ALU.mult, ALU.add)
+        elif name == "cpb":
+            act(full("cpb"), full(more[0]), ACT.Identity, bias=1.0, scale=-1.0)
+        elif name == "og":
+            tt(A("og", lo, hi), A("gpi", lo, hi), A(more[0], lo, hi), ALU.mult)
+        elif name == "sum0":
+            mm(full(more[0]), TRI, full("og"), False, True)
+        elif name == "sum1":
+            mm(full(more[0]), HEYE, full("cpb"), False, False)
+            mm(full(more[0]), TRI, full("og"), False, True)
+        elif name == "hc":
+            mm(full(more[0]), HEYE, full("cpb"), True, True)
+        elif name == "x0":
+            ts(A("x0", lo, hi), A(more[0], lo, hi), own + 256.0, None, ALU.add)
+        elif name == "u":
+            act(full("u" + more[0]), full(more[1]), ACT.Relu, bias=own + 256 + (0, 1, 3, 8)[int(more[0])] * BIG)
+        elif name == "last":
+            tt(A("x3", lo, hi), ind(full("x2"), A("l1", lo // 16, hi // 16)), A("u3", lo, hi), ALU.max)
+        elif name == "low12":
+            ts(A("x4", lo, hi), A("x3", lo, hi), 4095, None, ALU.bitwise_and)
+        elif name == "offs":
+            cp(A("soff", lo, hi), A("x4", lo, hi))
+        elif name == "half":
+            ts(A("s0", lo, hi), A("x4", lo, hi), -2048.0, None, ALU.add)
+        elif name == "back":
+            ts(A("soff", lo, hi), A(more[0], lo, hi), 2048.0, None, ALU.add)
+        elif name == "order":
+            place(more[0], "s0", lo, hi, True, True)
+        elif name == "gv":
+            h = int(more[0])
+            tt(piece("P", h), ind(table, A("soff", lo + 64 * h, lo + 64 * h + 64)), A("C8", 8 * lo, 8 * hi), ALU.subtract)
+        elif name == "gs":
+            act(A("P", 16 * lo, 16 * hi), ind(table, A("soff", lo, hi)), ACT.Copy)
+        elif name == "vg":
+            cp(A("P", 16 * lo, 16 * hi), ind(table, A("soff", lo, hi)))
+        elif name == "scan":
+            p, m, rm = links("P"), links("M"), A("RM", 0, 16 * n)
+            issue("v", lambda: g.vector.tensor_tensor_scan(m[0], rm[0], p[0], 0.0, ALU.min, ALU.max), regs(p, rm), regs(m))
+        elif name == "open":
+            mm(A("X", lo, hi), row("cm"), A("ones", 0, n, parts=1), True, False)
+            mid = lo + 128 if fused else lo
+            if fused:
+                mm(A("X", lo, mid), A("eye5", 0, 128), mine(r, lo, mid), False, False)
+            mm(A("X", mid, hi), EYE, mine(r, mid, hi), False, False)
+        elif name == "sum":
+            for b in range(4):
+                top = piece("M", b // 2, 4 * (b % 2) + 3, 8) if fused and not NATURAL else links("M", 4 * b + 3, 16)
+                mm(A("X", lo, hi), EYE, top, False, b == 3 and "end" in more)
+        elif name == "high":
+            act(A("yq", lo, hi), A("X", lo, hi), ACT.Identity, bias=-127.5)
+        elif name == "vhigh":
+            ts(A("yq", lo, hi), A("X", lo, hi), -127.5, None, ALU.add)
+        elif name == "low":
+            tt(mine(r + 1, lo, hi) if r < 2 else A("cout", lo, hi), A("X", lo, hi), A("yq", lo, hi), ALU.subtract)
+        elif name == "send":
+            if r < 2:
+                share("T%d" % (r + 1), lo, hi, "arr%d%s" % (r + 1, more[0]))
+            else:
+                store(T.yc[:, lo:hi], A("cout", lo, hi))
+        elif name == "crep":
+            for j in range(int(more[0]), 8, 2) if more else range(8):
+                select(A("C8", 8 * lo + j, 8 * hi, 8), mine(r + 1, lo, hi), [[0, n]], ALU.is_ge, 0, 0)
+        elif name == "wrap":
+            t = "T%d" % (r + 1)
+            select(A(t, 4096, 4098), A(t, 0, 2), [[0, 2]], ALU.is_ge, 0, 0)
+        elif name == "sub":
+            mm(full(more[1]), EYE, A("P", 16 * lo + int(more[0]), 16 * hi, 4), True, False)
+            for j in range(4):
+                mm(A(more[1], j, 512, 4), NEYE, mine(r, lo, hi), False, j == 3)
+        elif name == "pre":
+            mm(full(more[0]), row("zero"), A("ones", 0, V, parts=1), True, False)
+            for j in range(4):
+                mm(A(more[0], j, 512, 4), NEYE, mine(r, lo, hi), False, False)
+        elif name == "plus":
+            mm(full(more[1]), EYE, A("P", 16 * lo + int(more[0]), 16 * hi, 4), False, True)
+        elif name == "step":
+            step(piece("B", more[0]), full(more[1]))
+        elif name == "rep":
+            for j in range(4):
+                mm(A(more[0], j, 512, 4), EYE, mine(r, lo, hi), True, True)
+        elif name == "cmp":
+            tt(piece("B", more[0]), links("P", more[0], 4), full(more[1]), ALU.is_gt)
+        elif name == "bit":
+            ts(piece("B", more[0]) if more else links("B"), piece("P", more[0]) if more else links("P"), 0.0, None, ALU.is_gt)
+        elif name == "sbit":
+            step(piece("B", more[0]) if more else links("B"), piece("P", more[0]) if more else links("P"))
+        elif name == "cnt":
+            for c in range(lo // 8, hi // 8):
+                mm(A(more[0], c, c + 1), A("B", 128 * c, 128 * c + 128), A("ones", 0, 1), True, True)
+        elif name == "ft":
+            act(A("fts", lo // 8, hi // 8), A(more[0], lo // 8, hi // 8), ACT.Copy, scale=-1.0)
+        elif name == "vft":
+            ts(A("fts", lo // 8, hi // 8), A(more[0], lo // 8, hi // 8), -1.0, None, ALU.mult)
+        elif name == "spread":
+            for q in range(8):
+                mm(A(more[0], lo + q, hi, 8), A("spread", 128 * q, 128 * q + 128), A("fts", lo // 8, hi // 8), False, q == 7 and "more" not in more)
+        elif name == "thr":
+            mm(A(more[0], lo, hi), EYE, A("thc", lo, hi), True, False)
+        elif name == "add":
+            s, width = int(more[0]), 8 if fused and not NATURAL else 4
+            for j in range(width):
+                k = 8 * s + j if width == 8 else 4 * j + s
+                mm(A(more[1], lo, hi), A("en", 15 - k, 143 - k), links("B", k, 16) if NATURAL else piece("B", s, j, width), False,
+                   j == width - 1 and "end" in more)
+        elif name == "pass":
+            step(A(mb, lo, hi), A(more[0], lo, hi))
+        elif name == "vpass":
+            ts(A(mb, lo, hi), A(more[0], lo, hi), 0.5, None, ALU.is_gt)
+        elif name == "run":
+            mm(A("CM", lo, hi), TRI, A(mb, lo, hi), True, True)
+        elif name == "grow":
+            tt(A("y", lo, hi), A("CM", lo, hi), A("amp", lo, hi), ALU.min)
+        elif name == "base":
+            mm(A(more[0], lo, hi), EYE, A("s16", lo, hi), True, False)
+            place(more[0], "kst", lo, hi, False, False)
+        elif name == "t1":
+            act(A("t1", lo, hi), ind(full("y"), A("l1", lo // 16, hi // 16)), ACT.Copy, scale=0.5)
+        elif name == "t2":
+            act(A("t2", lo, hi), ind(full("y"), A("l23", lo // 16, hi // 16)), ACT.Copy, scale=0.25)
+        elif name == "vt2":
+            ts(A("t2", lo, hi), ind(full("y"), A("l23", lo // 16, hi // 16)), 0.25, None, ALU.mult)
+        elif name == "t3":
+            ts(A("t3", lo, hi), ind(full("y"), A("l23", 32 + lo // 16, 32 + hi // 16)), 0.11, 8.03085, ALU.mult, ALU.add)
+        elif name == "st3":
+            act(A("t3", lo, hi), ind(full("y"), A("l23", 32 + lo // 16, 32 + hi // 16)), ACT.Identity, bias=8.03085, scale=0.11)
+        elif name == "move":
+            for x in ("y", "t3", "t1", "t2"):
+                place(more[0], x, lo, hi, False, x == "t2")
+        elif name == "put":
+            place(more[1], more[0], lo, hi, False, "end" in more)
+        elif name == "fin":
+            ts(A("soff", lo, hi), A(more[0], lo, hi), ROUND, ROUND - 2040.0, ALU.add, ALU.subtract)
+        elif name == "gaps":
+            for j in range(3):
+                mm(A(more[0], lo, hi), row("ch"), A("ones", 0, n, parts=1), j == 0, False)
+                if j < 2:
+                    mm(A(more[0], lo, hi), A("fm", 0, 128), A("mb%d" % j, lo, hi), False, False)
+                    whole(more[0], lo, hi, False)
+        elif name == "val":
+            mm(A(more[0], lo, hi), A("fm", 0, 128), A(mb, lo, hi), True, True)
+        elif name == "inc":
+            act(A("inc%d" % r, lo, hi), A(more[0], lo, hi), ACT.Relu, scale=64.0)
+        elif name == "incs":
+            mm(A(more[0], lo, hi), row("ch"), A("ones", 0, n, parts=1), True, False)
+            for j in range(2):
+                mm(A(more[0], lo, hi), EYE, A("inc%d" % j, lo, hi), False, False)
+        elif name == "gap":
+            mm(A(more[0], lo, hi), A("fm", 0, 128), A(mb, lo, hi), False, False)
+            whole(more[0], lo, hi, True)
+        elif name == "out":
+            tt(A("gout", lo, hi), A(more[0], lo, hi), A("gpi", lo, hi), ALU.add)
+            store(T.yg[:, lo:hi], A("gout", lo, hi))
+        else:
+            raise ValueError(name)
+
+    load("y", mine(0, 0, V), T.c0[:], "ldc")
+    load("s", full("cpi"), T.cp[:], "ldp")
+    load("y", full("gpi"), T.gp[:], "ldg")
+    load("s", A("rfi", 0, 32), T.rf[:], "ldr")
+    iota(A("J", 0, 144), [[1, 144]], 0, -1)
+    iota(KS, [[16, 8], [0, 16]], 0, -1)
+    iota(full("pos"), [[1, V]], -256, 0)
+    for r in range(3):
+        for s in ROUNDS[r].split(";"):
+            w = s.split()
+            if not w or (":" in w[0] and w[0][0] != str(r)):
+                continue
+            w[0] = w[0].split(":")[-1]
+            named = len(w) > 1 and w[1] in PART
+            lo, hi = PART[w[1] if named else "all"]
+            run_step(r + w[0].count("+") - w[0].count("-"), w[0].strip("+-"), lo, hi, w[1 + named:])
+
     wait("g", "sent", total["sent"], {})
     for sem in ("qv", "qs", "qp", "qg", "st"):
         wait("y", sem, total[sem], {})

import math
from concourse.bass import DstId, RemoteDMATransfer
from concourse.mybir import AluOpType as ALU, AxisListType, ActivationFunctionType as ACT

V = 512
TW = 4096 + 16
HUGE = 4194304.0
ROUND = 12582912.0
BIG = 262144.0

BF, F16, F32, I32, U16 = "bfloat16", "float16", "float32", "int32", "uint16"
SBUF = {
    "T0": (TW, BF), "T1": (TW, BF), "T2": (TW, BF), "cout": (V, BF), "gout": (V, F32),
    "gpi": (V, I32), "cpi": (V, I32), "thi": (V, I32), "rfi": (32, I32),
    "P": (16 * V, BF), "M": (16 * V, BF), "B": (16 * V, BF), "C8": (8 * V, BF), "RM": (2048, BF),
    "J": (144, F32), "K": (128, F32), "pos": (V, BF),
    "eye": (128, BF), "neye": (128, BF), "heye": (128, BF), "eye5": (128, BF), "zs": (128, BF), "jge": (128, BF),
    "tri": (128, BF), "fw": (128, BF), "fm": (128, BF), "sel": (512, BF), "en": (144, BF), "spread": (1024, BF), "fts": (64, BF),
    "k0": (128, F32), "pm0": (8, F32), "wsel": (144, BF), "cm": (128, BF), "ch": (128, BF), "zero": (128, BF), "ones": (V, BF),
    "l1": (32, U16), "l23": (64, U16), "r1": (V, BF), "r23": (2 * V, BF),
    "cpb": (V, BF), "thc": (V, BF), "og": (V, F16), "cp1": (V, BF), "cp2": (V, BF), "kst": (V, BF), "amp": (V, BF),
    "x0": (V, F32), "x1": (V, F32), "x2": (V, F32), "x3": (V, I32), "x4": (V, I32), "u1": (V, F32), "u2": (V, F32), "u3": (V, F32),
    "soff": (V, U16), "s0": (V, F16), "s16": (V, F16), "yq": (V, BF),
    "inc0": (V, BF), "inc1": (V, BF), "mb0": (V, BF), "mb1": (V, BF), "mb2": (V, BF), "y": (V, BF), "t1": (V, BF), "t2": (V, BF), "t3": (V, BF),
}
PSUM = ["D0", "D1", "D2", "X", "FT", "F", "CM", "S0"]
SCRATCH = {k: ("sbuf", [128, SBUF[k][0]], SBUF[k][1]) for k in SBUF}
SCRATCH.update({k: ("psum", [128, 512], F32) for k in PSUM})
SEMAPHORES = ["qv", "qs", "qp", "qg", "ldc", "ldg", "ldp", "ldr", "ldt", "arr0", "arr1a", "arr1b", "arr1c", "arr2a", "arr2b", "arr2c",
              "sent", "st"]
COUNTER = {"v": "qv", "s": "qs", "p": "qp", "g": "qg"}

PART = {"A1": (0, 128), "B1": (128, 256), "B2": (256, 384), "A2": (384, 512), "a": (0, 256), "b": (256, 512), "all": (0, 512),
        "A1x": (0, 64), "A1y": (64, 128), "B1x": (128, 192), "B1y": (192, 256), "B2x": (256, 320), "B2y": (320, 384),
        "A2x": (384, 448), "A2y": (448, 512), "c": (0, 384), "B": (128, 384)}
ON_VECTOR = (0, 384)

START = ("jge; zs; mask; cm; eye5; eye; ones; neye; mask0; own X; tri; heye; l1; cpb X; og a X; og b X; pos D0; pos D1; first; sel; crep- A1; "
         "crep- A2; sum1 D1; sum0 D0; hop1; u 1 D1; u 2 D1; u 3 D1; hop2; cp1; k0; amp; pm0; x0 all D0; x1; x2; last a; low12 a; half A1; "
         "offs B1; hc F; order A1 S0; wsel; en; fin A1 S0; ")
STEPS = ("0:hop3; 0:cp2; 0:last b; 0:lists; 0:low12 b; gs B1; gv A1 0; 0:offs B2; 1:ch; 1:fin b D2; gv A1 1; 0:half A2; scan A1; scan B1; 0:thc; "
         "gs B2; scan B2; 0:order A2 S0; 0:fin A2 S0; 0:l23; sub B1 0 D0; open c; sub B1 1 D1; sum A1; 0:kst; step B1 0 D0; sbit A1 0; "
         "step B1 1 D1; sub B1 2 D0; sum B end; thr b FT; rep B2 D2; thr a F; high c; step B1 2 D0; sbit A1 1; gv A2 0; sub B1 3 D1; "
         "add B1 0 F; add A1 0 F; add B1 2 F; step B1 3 D1; add B1 1 F; add A1 1 F; add B1 3 F end; low c; cmp B2 0 D2; gv A2 1; cmp B2 2 D2; "
         "send c a; sbit A2 0; add B2 0 FT; add B2 2 FT; add A2 0 FT; scan A2; cmp B2 1 D2; cmp B2 3 D2; sbit A2 1; pass a F; open A2; "
         "sum A2 end; run a; high A2; 1:fw; add B2 1 FT; add B2 3 FT; add A2 1 FT end; low A2; s16; grow a; crep A1 0; send A2 b; crep A1 1; "
         "wrap; crep A2; pass b FT; base a S0; run b; base b D2; put a y S0; 1:fm; grow b; t1 a; t2 a; t3 a; put a t3 S0; put a t1 S0; "
         "put a t2 S0 end; t3 b; fin a S0; t1 b; t2 b; move b D2 ")
LAST = ("gv A1 0; fin b D2; gv A1 1; gs B1; gs B2; scan A1; gv A2 1; scan B1; scan B2; gv A2 0; open c; gaps a CM; sub B1 0 D0; rep B2 D2; "
        "sub B1 1 D1; gaps b S0; step B1 0 D0; step B1 1 D1; sum A1; thr b FT; sub B1 2 D0; thr a F; sub B1 3 D1; cmp B2 0 D2; sbit A1 0; "
        "step B1 2 D0; add B1 0 F; add A1 0 F; add B1 2 F; sum B end; sbit A1 1; add B1 1 F; add A1 1 F; cmp B2 2 D2; cmp B2 1 D2; cmp B2 3 D2; "
        "scan A2; sbit A2 0; add B2 0 FT; add B2 2 FT; add A2 0 FT; step B1 3 D1; add B1 3 F end; sbit A2 1; add B2 1 FT; high c; pass a F; "
        "add B2 3 FT; add A2 1 FT end; gap a CM; low c; send c a; out a CM; pass b FT; gap b S0; open A2; sum A2 end; high A2; out b S0; "
        "low A2; send A2 b ")
ON_VECTOR = (0,)
START = ("jge; zs; mask; ones; mask0; k0; eye5; heye; en; own X; tri; l1; eye; cpb X; og a X; og b X; amp; pm0; neye; pos D1; pos D0; sum1 D1; "
         "sum0 D0; hop1; u 1 D1; u 2 D1; u 3 D1; hop2; first; sel; crep- A1; cm; wsel; x0 all D0; x1; x2; last a; low12 a; half A1; offs B1; "
         "hop3; hc F; order A1 S0; lists; back A1 S0; ")
STEPS = ("1:ch; 0:last b; 0:low12 b; gv A1 1; 1:fin b D2; 0:offs b; gs B1; gs B2; rep B2 D2; open a; sub B1 0 D0; sub B1 3 CM; sub B1 1 D1; "
         "sub B1 2 S0; step B1 0 D0; gs A2; gv A1 0; bit A1 1; 0:l23; 0:thc; scan A1; bit A1 0; scan B1; cmp B2 0 D2; cmp B2 1 D2; cmp B2 2 D2; "
         "scan B2; thr a F; thr b FT; add A1 1 F; sub B2 3 D0; add B1 0 F; sum A1; sum B1 end; add A1 0 F; add B2 0 FT; rep A2 D2; add B2 2 FT; "
         "add B2 1 FT; high a; low a; step B1 1 D1; step B1 2 S0; step B2 3 D0; step B1 3 CM; add B1 1 F; open b; sum B2; cmp A2 0 D2; "
         "add A2 0 FT; add B1 2 F; add B2 3 FT; scan A2; cmp A2 1 D2; cmp A2 2 D2; cmp A2 3 D2; sum A2 end; add B1 3 F end; add A2 1 FT; high b; "
         "pass a F; 1:fw; add A2 2 FT; run a; add A2 3 FT end; low b; s16; grow a; pass b FT; run b; 1:fm; 0:kst; grow b; t3 a; send a a; "
         "crep A1 0; send b b; crep A1 1; wrap; t1 a; t2 a; t1 b; st3 b; t2 b; base a S0; base b D2; put a y S0; put a t1 S0; put a t3 S0; "
         "put a t2 S0 end; fin a S0; move b D2 ")
LAST = ("gs B1; gv A1 1; fin b D2; gv A1 0; gaps b S0; gaps a CM; bit A1 1; rep B2 D2; open a; bit A1 0; sub B1 1 D1; sub B1 0 D0; thr a F; "
        "thr b FT; add A1 0 F; add A1 1 F; gs B2; scan A1; step B1 1 D1; step B1 0 D0; scan B1; cmp B2 0 D2; cmp B2 1 D2; cmp B2 2 D2; scan B2; "
        "gs A2; add B1 1 F; sub B1 3 D1; sum A1; sub B1 2 D0; add B2 0 FT; add B2 1 FT; add B1 0 F; rep A2 D2; add B2 2 FT; sum B1 end; "
        "step B1 2 D0; cmp A2 0 D2; high a; step B1 3 D1; cmp A2 1 D2; low a; scan A2; cmp A2 2 D2; cmp A2 3 D2; add B1 2 F; sub B2 3 D0; "
        "step B2 3 D0; add A2 0 FT; add B1 3 F end; open b; sum B2; add A2 1 FT; sum A2 end; add B2 3 FT; add A2 2 FT; add A2 3 FT end; "
        "pass a F; high b; gap a CM; low b; send a a; send b b; out a CM; pass b FT; gap b S0; out b S0 ")
START = ("zs; jge; mask; eye5; en; k0; neye; ones; own X; heye; tri; l1; cm; cpb X; og a X; og b X; eye; pm0; mask0; wsel; first; sel; crep- A1; "
         "wide; pos D0; pos D1; sum1 D1; sum0 D0; hop1; u 1 D1; u 2 D1; hop2; u 3 D1; hop3; x0 all D0; x1; x2; last a; low12 a; half A1; offs B1; "
         "amp; hc F; lists; order A1 S0; back A1 S0; ")
STEPS = ("gs B1; 0:last b; 0:l23; 0:low12 b; gv A1 0; 0:offs b; 1:fin b D2; open a; rep B2 D2; sub B1 2 S0; sub B1 1 D1; sub B1 0 D0; "
         "sub B1 3 CM; gv A1 1; scan B1; scan A1; sum a end; gs B2; step B1 0 D0; high a; 0:thc; bit A1; cmp B2 0 D2; low a; sub B2 3 D0; "
         "cmp B2 1 D2; cnt A1 FT; vft A1 FT; thr c F; open b; cmp B2 2 D2; scan B2; gs A2; scan A2; step B1 1 D1; step B1 2 S0; step B2 3 D0; "
         "step B1 3 CM; spread A1 F more; add B2 0 F; add B2 1 F; add B1 0 F; rep A2 D2; add B2 2 F; add B1 1 F; thr A2 D1; add B1 2 F; "
         "sum b end; add B2 3 F; add B1 3 F end; high b; 1:fw; pass c F; cmp A2 0 D2; cmp A2 1 D2; cmp A2 2 D2; low b; cmp A2 3 D2; send a a; "
         "crep A1 1; send b b; wrap; crep A1 0; add A2 1 D1; add A2 0 D1; add A2 2 D1; run c; s16; grow c; add A2 3 D1 end; pass A2 D1; run A2; "
         "0:kst; 1:fm; grow A2; 1:ch; t3 a; t3 b; base a S0; put a y S0; t1 a; t2 a; put a t1 S0; put a t3 S0; put a t2 S0 end; base b D2; t2 b; "
         "t1 b; fin a S0; move b D2 ")
LAST = ("gs B1; gv A1 0; fin b D2; gv A1 1; gs B2; bit A1; gaps c CM; rep B2 D2; thr c F; sub B1 1 D1; open a; sub B1 0 D0; gaps A2 S0; "
        "cnt A1 FT; step B1 0 D0; sub B1 2 D0; scan B1; vft A1 FT; cmp B2 0 D2; scan A1; cmp B2 1 D2; cmp B2 2 D2; scan B2; step B1 1 D1; "
        "spread A1 F more; sub B1 3 D1; add B2 0 F; add B1 1 F; sum a end; add B1 0 F; add B2 1 F; gs A2; step B1 2 D0; add B2 2 F; rep A2 D2; "
        "sub B2 3 D0; step B1 3 D1; high a; step B2 3 D0; cmp A2 0 D2; low a; cmp A2 1 D2; cmp A2 2 D2; scan A2; cmp A2 3 D2; add B1 2 F; "
        "thr A2 D1; add A2 0 D1; add B2 3 F; add B1 3 F end; pass c F; open b; add A2 1 D1; add A2 2 D1; gap c CM; sum b end; add A2 3 D1 end; "
        "high b; pass A2 D1; gap A2 S0; send a a; out c CM; low b; send b b; out A2 S0 ")
START = ("jge; zs; cm; mask; k0; heye; eye5; ones; own X; pm0; eye; tri; l1; cpb X; og a X; og b X; amp; mask0; neye; first; sel; crep- A1; "
         "pos D0; pos D1; sum1 D1; sum0 D0; hop1; u 1 D1; u 2 D1; u 3 D1; hop2; hop3; x0 all D0; x1; x2; last a; last b; low12 a; low12 b; "
         "half A1; offs B1; order A1 S0; hc F; offs b; back A1 S0; ")
STEPS = ("gs B1; 0:wsel; gv A1 0; 1:fin b D2; gv A1 1; scan B1; scan A1; 0:thc; 0:en; bit A1; 0:lists; open a; rep B2 D2; sub B1 1 D1; "
         "sub B1 2 S0; sub B1 3 CM; sub B1 0 D0; sum A1; sum B1 end; gs B2; step B1 0 D0; high a; gs A2; step B1 1 D1; step B1 2 S0; cmp B2 0 D2; "
         "low a; cmp B2 1 D2; cmp B2 2 D2; scan B2; thr c F; add B1 0 F; sub B2 3 D0; add A1 1 F; add A1 0 F; add B2 0 F; add B2 1 F; add B2 2 F; "
         "open b; rep A2 D2; add B1 1 F; add B1 2 F; scan A2; sum b end; cmp A2 0 D2; step B2 3 D0; add B2 3 F; step B1 3 CM; add B1 3 F end; "
         "thr A2 D1; high b; 1:fw; pass c F; cmp A2 1 D2; cmp A2 2 D2; low b; send a a; crep A1 1; send b b; wrap; crep A1 0; add A2 1 D1; "
         "add A2 2 D1; run c; add A2 0 D1; cmp A2 3 D2; grow c; 1:ch; s16; 0:kst; add A2 3 D1 end; pass A2 D1; run A2; grow A2; 0:l23; 1:fm; "
         "t3 a; t3 b; t1 a; t2 a; base B1 D0; put B1 y D0; base A1 S0; put A1 y S0; put B1 t1 D0; put A1 t1 S0; put B1 t3 D0; put A1 t3 S0; "
         "put B1 t2 D0 end; put A1 t2 S0 end; base b D2; t2 b; t1 b; fin B1 D0; fin A1 S0; move b D2 ")
LAST = ("gs B1; gv A1 0; fin b D2; gv A1 1; gs B2; bit A1; gaps A2 S0; gaps c CM; thr c F; sub B1 1 D1; open a; rep B2 D2; sub B1 0 D0; "
        "step B1 0 D0; step B1 1 D1; scan A1; cmp B2 0 D2; cmp B2 1 D2; cmp B2 2 D2; scan B1; scan B2; add A1 1 F; add A1 0 F; sub B1 2 D0; "
        "sub B1 3 D1; add B1 1 F; add B2 0 F; rep A2 D2; add B1 0 F; sum A1; add B2 1 F; sum B1 end; add B2 2 F; gs A2; step B1 2 D0; "
        "sub B2 3 D0; high a; step B1 3 D1; cmp A2 0 D2; add B1 2 F; low a; cmp A2 1 D2; thr A2 D1; add A2 0 D1; open b; scan A2; step B2 3 D0; "
        "add B2 3 F; add B1 3 F end; add A2 1 D1; cmp A2 2 D2; cmp A2 3 D2; pass c F; sum b end; gap c CM; add A2 2 D1; add A2 3 D1 end; high b; "
        "pass A2 D1; gap A2 S0; send a a; low b; send b b; out c CM; out A2 S0 ")
START = ("mask; mask0; ones; heye; cm; own X; zs; jge; tri; neye; cpb X; eye5; l1; og a X; og b X; k0; amp; eye; pm0; first; sel; crep- A1; "
         "pos D0; pos D1; sum1 D1; sum0 D0; x0 all D0; hop1; u 1 D1; u 2 D1; u 3 D1; hop2; hop3; x1; x2; last a; last b; low12 a; low12 b; "
         "half A1; offs B1; offs b; order A1 S0; hc F; back A1 S0; ")
STEPS = ("gs B1; 0:en; 0:wsel; gv A1 0; 1:fin b D2; gv A1 1; open a; rep B2 D2; 0:lists; scan B1; scan A1; 0:thc; bit A1; gs B2; cmp B2 0 D2; "
         "sub B1 1 D1; sub B1 2 S0; sub B1 0 D0; sub B1 3 CM; sum A1; sum B1 end; step B1 1 D1; thr c F; thr A2 D1; add B1 1 F; high a; gs A2; "
         "step B1 2 S0; step B1 0 D0; step B1 3 CM; low a; cmp B2 1 D2; add A1 1 F; open b; add A1 0 F; cmp B2 2 D2; cmp B2 3 D2; scan B2; 0:l23; "
         "add B2 2 F; rep A2 D2; add B2 3 F; add B2 0 F; add B2 1 F; add B1 2 F; add B1 0 F; scan A2; cmp A2 0 D2; cmp A2 1 D2; sum b end; "
         "add B1 3 F end; add A2 1 D1; add A2 0 D1; high b; pass c F; 1:fw; cmp A2 2 D2; low b; cmp A2 3 D2; s16; 0:kst; run c; add A2 2 D1; "
         "add A2 3 D1 end; grow c; pass A2 D1; base A1 S0; run A2; send a a; crep A1 1; send b b; wrap; crep A1 0; put A1 y S0; base B1 D0; "
         "put B1 y D0; base b D2; 1:fm; grow A2; t1 a; 1:ch; t3 a; t3 b; t2 a; put A1 t1 S0; put B1 t3 D0; put B1 t1 D0; put B1 t2 D0 end; "
         "put A1 t3 S0; t1 b; t2 b; put A1 t2 S0 end; fin B1 D0; fin A1 S0; move b D2 ")
LAST = ("gs B1; gv A1 0; fin b D2; gv A1 1; gs B2; bit A1; gaps c CM; thr c F; open a; gaps A2 S0; sub B1 0 D0; rep B2 D2; scan A1; cmp B2 0 D2; "
        "cmp B2 1 D2; cmp B2 2 D2; sub B1 1 D1; add A1 1 F; add A1 0 F; step B1 0 D0; step B1 1 D1; gs A2; cmp B2 3 D2; scan B1; scan B2; "
        "sum A1; sub B1 2 D0; sub B1 3 D1; add B2 1 F; add B2 2 F; rep A2 D2; add B1 0 F; sum B1 end; add B2 3 F; add B1 1 F; add B2 0 F; "
        "step B1 3 D1; thr A2 D1; cmp A2 0 D2; cmp A2 1 D2; high a; step B1 2 D0; low a; add A2 0 D1; add A2 1 D1; add B1 2 F; add B1 3 F end; "
        "open b; scan A2; sum b end; cmp A2 2 D2; pass c F; high b; gap c CM; add A2 2 D1; cmp A2 3 D2; low b; add A2 3 D1 end; pass A2 D1; "
        "gap A2 S0; send a a; send b b; out c CM; out A2 S0 ")
START = ("zs; jge; cm; mask; heye; k0; neye; ones; own X; cpb X; tri; l1; pm0; eye5; og a X; og b X; mask0; eye; first; sel; crep- A1; pos D0; "
         "pos D1; sum1 D1; sum0 D0; hop1; u 1 D1; u 2 D1; u 3 D1; hop2; samp; hop3; x0 all D0; x1; x2; last a; last b; low12 a; low12 b; half A1; "
         "order A1 S0; hc F; offs B1; offs b; back A1 S0; ")
STEPS = ("0:en; 0:wsel; gv A1 0; 1:fin b D2; gv A1 1; 0:fw; gs B1; scan B1; open a; 1:val- all FT; 0:lists; rep B2 D2; sub B1 1 D1; sub B1 3 CM; "
         "sub B1 0 D0; sub B1 2 S0; gs B2; scan A1; 0:thc; bit A1; cmp B2 0 D2; sum A1; sum B1 end; step B1 1 D1; high a; gs A2; step B1 2 S0; "
         "step B1 0 D0; low a; cmp B2 1 D2; cmp B2 2 D2; cmp B2 3 D2; scan B2; 0:kst; scan A2; thr c F; add B1 1 F; thr A2 D1; add A1 0 F; "
         "add A1 1 F; add B2 1 F; open b; add B2 2 F; rep A2 D2; add B2 0 F; add B2 3 F; add B1 2 F; cmp A2 0 D2; cmp A2 1 D2; cmp A2 2 D2; "
         "add B1 0 F; sum b end; step B1 3 CM; high b; add B1 3 F end; add A2 0 D1; pass c F; 1:inc- all FT; add A2 1 D1; run c; add A2 2 D1; "
         "low b; cmp A2 3 D2; s16; grow c; add A2 3 D1 end; pass A2 D1; send a a; crep A1 0; crep A1 1; send b b; wrap; base A1 S0; run A2; "
         "base B1 D0; base b D2; put B1 y D0; put A1 y S0; 0:l23; grow A2; 0:fm; t3 a; t1 a; put A1 t1 S0; put B1 t1 D0; put B1 t3 D0; t2 a; "
         "put B1 t2 D0 end; put A1 t3 S0; put A1 t2 S0 end; t3 b; fin B1 D0; 1:ch; fin A1 S0; t2 b; t1 b; move b D2 ")
LAST = ("gs B1; gv A1 1; fin b D2; gv A1 0; gs B2; thr c F; open a; val- all FT; rep B2 D2; sub B1 3 CM; sub B1 0 D0; sub B1 2 S0; sub B1 1 D1; "
        "bit A1; scan B1; cmp B2 0 D2; cmp B2 1 D2; cmp B2 2 D2; cmp B2 3 D2; step B1 0 D0; step B1 2 S0; step B1 1 D1; step B1 3 CM; gs A2; "
        "inc- all FT; scan A1; scan B2; add A1 1 F; add B1 0 F; add A1 0 F; add B1 2 F; add B1 1 F; thr A2 D1; add B2 1 F; add B2 2 F; "
        "add B2 0 F; add B2 3 F; rep A2 D2; sum A1; sum B1 end; add B1 3 F end; incs c CM; cmp A2 0 D2; high a; pass c F; cmp A2 1 D2; low a; "
        "scan A2; add A2 0 D1; add A2 1 D1; gap c CM; open b; sum b end; cmp A2 2 D2; add A2 2 D1; high b; send a a; cmp A2 3 D2; out c CM; "
        "low b; send b b; add A2 3 D1 end; incs A2 S0; pass A2 D1; gap A2 S0; out A2 S0 ")
ROUNDS = [START + STEPS, STEPS, LAST]
NATURAL = False


def rank_program(g, core, T, topo):
    rank = T.rank_of(core)
    if rank is None:
        return
    n_ranks = len(T.cores)
    own = V * rank
    queue = {"v": g.vector, "s": g.scalar, "p": g.tensor, "g": g, "y": g.sync}
    touches = {}
    known = {q: {} for q in queue}
    total = {}

    def A(name, lo, hi, step=1, parts=None):
        t = T[name]
        if parts is not None:
            ap = t[0:parts, lo:hi:step] if step > 1 else t[0:parts, lo:hi]
        elif step > 1:
            ap = t[:, lo:hi:step]
        else:
            ap = t[:, lo:hi]
        return ap, (name, lo, hi, step)

    def meet(a, b):
        return a[1] < b[1] and b[0] < a[2] and (a[1] - b[0]) % math.gcd(a[3], b[2]) == 0

    def wait(q, sem, count, seen):
        if known[q].get(sem, 0) >= count:
            return
        queue[q].wait_ge(T.sem[sem], count)
        known[q][sem] = count
        for s, c in seen.items():
            if known[q].get(s, 0) < c:
                known[q][s] = c

    def note(q, reads, writes, mark):
        for rs, w in ((reads, False), (writes, True)):
            for r in rs:
                old = touches.get(r[0], [])
                if r[0] in PSUM:
                    old = [] if q == "p" else old
                elif w and r[3] == 1:
                    old = [x for x in old if not (r[1] <= x[0] and x[1] <= r[2])]
                touches[r[0]] = old + [(r[1], r[2], r[3], w, q, mark)]

    def issue(q, call, reads, writes, sem=None, count=1, after=()):
        need = {}
        marks = list(after)
        for rs, w in ((reads, False), (writes, True)):
            for r in rs:
                for x in touches.get(r[0], []):
                    if (x[4] != q or (q != "p" and (w or x[3]))) if r[0] in PSUM else ((w or x[3]) and meet(r, x)):
                        marks.append(x[5])
        for s, c, seen in marks:
            if c > need.get(s, (0, None))[0]:
                need[s] = (c, seen)
        for s in sorted(need, key=lambda s: s == COUNTER.get(q)):
            wait(q, s, need[s][0], need[s][1])
        ins = call()
        sem = sem or COUNTER[q]
        if ins is not None:
            ins.then_inc(T.sem[sem], count)
        total[sem] = total.get(sem, 0) + count
        mark = (sem, total[sem], dict(known[q]))
        note(q, reads, writes, mark)
        return mark

    def ind(win, off):
        return win[0].indirect(off[0]), win[1], off[1]

    def regs(*xs):
        return [r for x in xs if isinstance(x, tuple) for r in x[1:]]

    def val(x):
        return x[0] if isinstance(x, tuple) else x

    def ts(out, a, s1, s2, op0, op1=None):
        if op1 is None:
            call = lambda: g.vector.tensor_scalar(out[0], a[0], val(s1), None, op0)
        else:
            call = lambda: g.vector.tensor_scalar(out[0], a[0], val(s1), val(s2), op0, op1)
        issue("v", call, regs(a, s1, s2), regs(out))

    def tt(out, a, b, o):
        issue("v", lambda: g.vector.tensor_tensor(out[0], a[0], b[0], o), regs(a, b), regs(out))

    def cp(out, a):
        issue("v", lambda: g.vector.tensor_copy(out[0], a[0]), regs(a), regs(out))

    def fill(out, c):
        issue("v", lambda: g.vector.memset(out[0], c), [], regs(out))

    def act(out, a, func, bias=0.0, scale=1.0):
        issue("s", lambda: g.scalar.activation(out[0], a[0], func, bias=bias, scale=scale), regs(a), regs(out))

    def step(out, a):
        act(out, a, ACT.Sigmoid, bias=-128.0, scale=256.0)

    def mm(out, lhs, rhs, start, stop):
        issue("p", lambda: g.tensor.matmul(out[0], lhs[0], rhs[0], start, stop), regs(lhs, rhs), regs(out))

    def iota(out, pattern, base, mult):
        issue("g", lambda: g.iota(out[0], pattern, base, mult, allow_small_or_imprecise_dtypes=True), [], regs(out))

    def select(out, a, pattern, op, base, mult):
        issue("g", lambda: g.affine_select(out[0], a[0], pattern, op, 0.0, base, mult), regs(a), regs(out))

    def load(q, out, src, sem, after=()):
        issue(q, lambda: queue[q].dma_start(out[0], src), [], regs(out), sem, 16, after)

    def store(dst, a):
        issue("y", lambda: g.sync.dma_start(dst, a[0]), regs(a), [], "st", 16)

    others = [T.cores[(rank + d) % n_ranks] for d in range(1, n_ranks)]
    mask = topo.mask(core, others[0])
    for o in others:
        mask &= topo.mask(core, o)
    n_eng = bin(mask).count("1")
    ids = [DstId(rid=topo.addr(o)[0], pnc=topo.addr(o)[1]) for o in others]

    def share(table, lo, hi, arr):
        src = A(table, own + lo, own + hi)

        def call():
            g.remote_dma_fused([RemoteDMATransfer(dst_ids=ids, dma_engine_mask=mask, remote_sem=T.sem[arr], srcs=[src[0]],
                                                  dsts=[src[0] for o in others])], local_sem=T.sem["sent"])
        issue("g", call, regs(src), [], "sent", n_eng)
        mark = (arr, n_eng * (n_ranks - 1), {})
        note("far", [], [(table, V * r + lo, V * r + hi, 1) for r in range(n_ranks) if r != rank], mark)
        return mark

    EYE, NEYE, HEYE, TRI = A("eye", 0, 128), A("neye", 0, 128), A("heye", 0, 128), A("tri", 0, 128)
    JS, KS, L1 = A("J", 0, 128), A("K", 0, 128), A("l1", 0, 32)

    def full(name):
        return A(name, 0, V)

    def mine(r, lo, hi):
        return A("T%d" % r, own + lo, own + hi)

    def row(name):
        return A(name, 0, 128, parts=1)

    def whole(bank, lo, hi, stop):
        mm(A(bank, lo, hi), row("cm"), A("RM", 1, 4 * (hi - lo), 4, parts=1), False, False)
        mm(A(bank, lo, hi), row("cm"), A("RM", 0, 4 * (hi - lo), 4, parts=1), False, stop)

    def place(bank, name, lo, hi, start, stop):
        a = lo
        while a < hi:
            b = a + 128 if a in ON_VECTOR else min([x for x in ON_VECTOR if x > a] + [hi])
            end = stop and b == hi
            if a in ON_VECTOR:
                for j in range(4):
                    h, q = j // 2, j % 2
                    mm(A(bank, a + 64 * h, a + 64 * h + 64), A("sel", 128 * j, 128 * j + 128), A(name, a + q, b, 2),
                       start and q == 0, (start and q == 1) or (end and j == 3))
            else:
                mm(A(bank, a, b), EYE, A(name, a, b), start, end)
            a = b

    def sigmoid(out, a, sign):
        act(out, a, ACT.Sigmoid, bias=128.0, scale=256.0 * sign)

    def lists():
        for q in range(16):
            mm(A("FT", 0, 64), A("wsel", 15 - q, 143 - q), A("r23", q, 2 * V, 16), q == 0, q == 15)

    def first():
        load("y", full("thi"), T.th[:], "ldt", [share("T0", 0, V, "arr0")])

    def sel():
        for j in range(4):
            select(A("sel", 128 * j, 128 * j + 128), A("ones", 0, 128), [[-16, 8], [1000, 2], [-2 if NATURAL else -1, 8]], ALU.is_equal,
                   -(1 if NATURAL else 8) * (j // 2) - 1000 * (j % 2), 1)

    def wide():
        for j in range(2):
            select(A("spread", V * j, V * j + V), full("ones"), [[-16, 4], [0, 8], [-1, 16]], ALU.is_equal, -64 * j, 1)

    def en():
        fill(A("en", 0, 144), 0.0)
        fill(A("en", 15, 144, 16), -1.0)

    single = {
        "mask": lambda: fill(A("RM", 0, 2048), 256.0), "mask0": lambda: fill(A("RM", 0, 2048, 4), -256.0),
        "ones": lambda: fill(full("ones"), 1.0), "cm": lambda: fill(row("cm"), 49152.0), "zero": lambda: fill(row("zero"), 0.0), "ch": lambda: fill(row("ch"), 63.0 / 128),
        "jge": lambda: sigmoid(A("jge", 0, 128), JS, 1), "zs": lambda: sigmoid(A("zs", 0, 128), KS, -1),
        "heye": lambda: ts(HEYE, JS, 0.0, -HUGE, ALU.is_equal, ALU.mult), "eye": lambda: ts(EYE, JS, 0.0, None, ALU.is_equal),
        "neye": lambda: ts(NEYE, JS, 0.0, -1.0, ALU.is_equal, ALU.mult),
        "eye5": lambda: ts(A("eye5", 0, 128), JS, 0.0, 5.0, ALU.is_equal, ALU.mult),
        "tri": lambda: tt(TRI, A("jge", 0, 128), A("zs", 0, 128), ALU.mult),
        "k0": lambda: ts(A("k0", 0, 128), KS, 0.0, None, ALU.is_equal),
        "pm0": lambda: issue("v", lambda: g.vector.tensor_reduce(T.pm0[:, 0:1], T.k0[:, 0:128], AxisListType.X, ALU.max),
                             [("k0", 0, 128, 1)], [("pm0", 0, 1, 1)]),
        "wsel": lambda: ts(A("wsel", 0, 144), A("J", 0, 144), 15.0, A("pm0", 0, 1), ALU.is_equal, ALU.mult),
        "fw": lambda: act(A("fw", 0, 128), EYE, ACT.Identity, bias=-1.0 / 32, scale=3.0 / 64),
        "fm": lambda: tt(A("fm", 0, 128), TRI, A("fw", 0, 128), ALU.mult),
        "first": first, "sel": sel, "en": en, "lists": lists, "wide": wide,
        "l1": lambda: cp(L1, A("rfi", 0, 32)), "l23": lambda: ts(A("l23", 0, 64), A("FT", 0, 64), 256.0, None, ALU.add),
        "hop1": lambda: act(full("r1"), ind(full("pos"), L1), ACT.Copy),
        "hop2": lambda: act(A("r23", 0, V), ind(full("r1"), L1), ACT.Copy),
        "hop3": lambda: act(A("r23", V, 2 * V), ind(A("r23", 0, V), L1), ACT.Copy),
        "cp1": lambda: act(full("cp1"), ind(full("cpb"), L1), ACT.Copy, scale=0.5),
        "x1": lambda: tt(full("x1"), ind(full("x0"), L1), full("u1"), ALU.max),
        "x2": lambda: tt(full("x2"), ind(full("x1"), L1), full("u2"), ALU.max),
        "thc": lambda: tt(full("thc"), full("thi"), full("F"), ALU.add),
        "kst": lambda: ts(full("kst"), full("x3"), -0.055 / BIG, 0.46, ALU.mult, ALU.add),
        "amp": lambda: ts(full("amp"), full("cpb"), -63.0 / 128, 0.5, ALU.mult, ALU.add),
        "samp": lambda: act(full("amp"), full("cpb"), ACT.Identity, bias=0.5, scale=-63.0 / 128),
        "s16": lambda: ts(full("s16"), full("soff"), -2048.0, None, ALU.add),
    }

    def run_step(r, name, lo, hi, more):
        n = hi - lo
        mb = "mb%d" % r
        table = A("T%d" % max(r, 0), 0, 4096 + (2 if r else 0))
        fused = lo - lo % 128 in ON_VECTOR

        def links(name, first=0, step=1):
            return A(name, 16 * lo + int(first), 16 * hi, int(step))

        def piece(name, s, first=0, step=1):
            if NATURAL:
                return links(name, s, 2 if fused else 4)
            at, width = (1024 * int(s), 8) if fused else (2048 + 1536 * int(s) + 4 * (lo - 128), 4)
            return A(name, at + first, at + width * n, step)

        if name in single:
            single[name]()
        elif name == "pos":
            mm(full(more[0]), row("ones"), A("pos", 0, V, parts=1), True, False)
        elif name == "own":
            ts(full(more[0]), full("cpi"), -1.0, 1.0, ALU.mult, ALU.add)
        elif name == "cpb":
            act(full("cpb"), full(more[0]), ACT.Identity, bias=1.0, scale=-1.0)
        elif name == "og":
            tt(A("og", lo, hi), A("gpi", lo, hi), A(more[0], lo, hi), ALU.mult)
        elif name == "sum0":
            mm(full(more[0]), TRI, full("og"), False, True)
        elif name == "sum1":
            mm(full(more[0]), HEYE, full("cpb"), False, False)
            mm(full(more[0]), TRI, full("og"), False, True)
        elif name == "hc":
            mm(full(more[0]), HEYE, full("cpb"), True, True)
        elif name == "x0":
            ts(A("x0", lo, hi), A(more[0], lo, hi), own + 256.0, None, ALU.add)
        elif name == "u":
            act(full("u" + more[0]), full(more[1]), ACT.Relu, bias=own + 256 + (0, 1, 3, 8)[int(more[0])] * BIG)
        elif name == "last":
            tt(A("x3", lo, hi), ind(full("x2"), A("l1", lo // 16, hi // 16)), A("u3", lo, hi), ALU.max)
        elif name == "low12":
            ts(A("x4", lo, hi), A("x3", lo, hi), 4095, None, ALU.bitwise_and)
        elif name == "offs":
            cp(A("soff", lo, hi), A("x4", lo, hi))
        elif name == "half":
            ts(A("s0", lo, hi), A("x4", lo, hi), -2048.0, None, ALU.add)
        elif name == "back":
            ts(A("soff", lo, hi), A(more[0], lo, hi), 2048.0, None, ALU.add)
        elif name == "order":
            place(more[0], "s0", lo, hi, True, True)
        elif name == "gv":
            h = int(more[0])
            tt(piece("P", h), ind(table, A("soff", lo + 64 * h, lo + 64 * h + 64)), A("C8", 8 * lo, 8 * hi), ALU.subtract)
        elif name == "gs":
            act(A("P", 16 * lo, 16 * hi), ind(table, A("soff", lo, hi)), ACT.Copy)
        elif name == "vg":
            cp(A("P", 16 * lo, 16 * hi), ind(table, A("soff", lo, hi)))
        elif name == "scan":
            p, m, rm = links("P"), links("M"), A("RM", 0, 16 * n)
            issue("v", lambda: g.vector.tensor_tensor_scan(m[0], rm[0], p[0], 0.0, ALU.min, ALU.max), regs(p, rm), regs(m))
        elif name == "open":
            mm(A("X", lo, hi), row("cm"), A("ones", 0, n, parts=1), True, False)
            mid = lo + 128 if fused else lo
            if fused:
                mm(A("X", lo, mid), A("eye5", 0, 128), mine(r, lo, mid), False, False)
            mm(A("X", mid, hi), EYE, mine(r, mid, hi), False, False)
        elif name == "sum":
            for b in range(4):
                top = piece("M", b // 2, 4 * (b % 2) + 3, 8) if fused and not NATURAL else links("M", 4 * b + 3, 16)
                mm(A("X", lo, hi), EYE, top, False, b == 3 and "end" in more)
        elif name == "high":
            act(A("yq", lo, hi), A("X", lo, hi), ACT.Identity, bias=-127.5)
        elif name == "vhigh":
            ts(A("yq", lo, hi), A("X", lo, hi), -127.5, None, ALU.add)
        elif name == "low":
            tt(mine(r + 1, lo, hi) if r < 2 else A("cout", lo, hi), A("X", lo, hi), A("yq", lo, hi), ALU.subtract)
        elif name == "send":
            if r < 2:
                share("T%d" % (r + 1), lo, hi, "arr%d%s" % (r + 1, more[0]))
            else:
                store(T.yc[:, lo:hi], A("cout", lo, hi))
        elif name == "crep":
            for j in range(int(more[0]), 8, 2) if more else range(8):
                select(A("C8", 8 * lo + j, 8 * hi, 8), mine(r + 1, lo, hi), [[0, n]], ALU.is_ge, 0, 0)
        elif name == "wrap":
            t = "T%d" % (r + 1)
            select(A(t, 4096, 4098), A(t, 0, 2), [[0, 2]], ALU.is_ge, 0, 0)
        elif name == "sub":
            mm(full(more[1]), EYE, A("P", 16 * lo + int(more[0]), 16 * hi, 4), True, False)
            for j in range(4):
                mm(A(more[1], j, 512, 4), NEYE, mine(r, lo, hi), False, j == 3)
        elif name == "pre":
            mm(full(more[0]), row("zero"), A("ones", 0, V, parts=1), True, False)
            for j in range(4):
                mm(A(more[0], j, 512, 4), NEYE, mine(r, lo, hi), False, False)
        elif name == "plus":
            mm(full(more[1]), EYE, A("P", 16 * lo + int(more[0]), 16 * hi, 4), False, True)
        elif name == "step":
            step(piece("B", more[0]), full(more[1]))
        elif name == "rep":
            for j in range(4):
                mm(A(more[0], j, 512, 4), EYE, mine(r, lo, hi), True, True)
        elif name == "cmp":
            tt(piece("B", more[0]), links("P", more[0], 4), full(more[1]), ALU.is_gt)
        elif name == "bit":
            ts(piece("B", more[0]) if more else links("B"), piece("P", more[0]) if more else links("P"), 0.0, None, ALU.is_gt)
        elif name == "sbit":
            step(piece("B", more[0]) if more else links("B"), piece("P", more[0]) if more else links("P"))
        elif name == "cnt":
            for c in range(lo // 8, hi // 8):
                mm(A(more[0], c, c + 1), A("B", 128 * c, 128 * c + 128), A("ones", 0, 1), True, True)
        elif name == "ft":
            act(A("fts", lo // 8, hi // 8), A(more[0], lo // 8, hi // 8), ACT.Copy, scale=-1.0)
        elif name == "vft":
            ts(A("fts", lo // 8, hi // 8), A(more[0], lo // 8, hi // 8), -1.0, None, ALU.mult)
        elif name == "spread":
            for q in range(8):
                mm(A(more[0], lo + q, hi, 8), A("spread", 128 * q, 128 * q + 128), A("fts", lo // 8, hi // 8), False, q == 7 and "more" not in more)
        elif name == "thr":
            mm(A(more[0], lo, hi), EYE, A("thc", lo, hi), True, False)
        elif name == "add":
            s, width = int(more[0]), 8 if fused and not NATURAL else 4
            for j in range(width):
                k = 8 * s + j if width == 8 else 4 * j + s
                mm(A(more[1], lo, hi), A("en", 15 - k, 143 - k), links("B", k, 16) if NATURAL else piece("B", s, j, width), False,
                   j == width - 1 and "end" in more)
        elif name == "pass":
            step(A(mb, lo, hi), A(more[0], lo, hi))
        elif name == "vpass":
            ts(A(mb, lo, hi), A(more[0], lo, hi), 0.5, None, ALU.is_gt)
        elif name == "run":
            mm(A("CM", lo, hi), TRI, A(mb, lo, hi), True, True)
        elif name == "grow":
            tt(A("y", lo, hi), A("CM", lo, hi), A("amp", lo, hi), ALU.min)
        elif name == "base":
            mm(A(more[0], lo, hi), EYE, A("s16", lo, hi), True, False)
            place(more[0], "kst", lo, hi, False, False)
        elif name == "t1":
            act(A("t1", lo, hi), ind(full("y"), A("l1", lo // 16, hi // 16)), ACT.Copy, scale=0.5)
        elif name == "t2":
            act(A("t2", lo, hi), ind(full("y"), A("l23", lo // 16, hi // 16)), ACT.Copy, scale=0.25)
        elif name == "vt2":
            ts(A("t2", lo, hi), ind(full("y"), A("l23", lo // 16, hi // 16)), 0.25, None, ALU.mult)
        elif name == "t3":
            ts(A("t3", lo, hi), ind(full("y"), A("l23", 32 + lo // 16, 32 + hi // 16)), 0.11, 8.03085, ALU.mult, ALU.add)
        elif name == "st3":
            act(A("t3", lo, hi), ind(full("y"), A("l23", 32 + lo // 16, 32 + hi // 16)), ACT.Identity, bias=8.03085, scale=0.11)
        elif name == "move":
            for x in ("y", "t3", "t1", "t2"):
                place(more[0], x, lo, hi, False, x == "t2")
        elif name == "put":
            place(more[1], more[0], lo, hi, False, "end" in more)
        elif name == "fin":
            ts(A("soff", lo, hi), A(more[0], lo, hi), ROUND, ROUND - 2040.0, ALU.add, ALU.subtract)
        elif name == "gaps":
            for j in range(3):
                mm(A(more[0], lo, hi), row("ch"), A("ones", 0, n, parts=1), j == 0, False)
                if j < 2:
                    mm(A(more[0], lo, hi), A("fm", 0, 128), A("mb%d" % j, lo, hi), False, False)
                    whole(more[0], lo, hi, False)
        elif name == "val":
            mm(A(more[0], lo, hi), A("fm", 0, 128), A(mb, lo, hi), True, True)
        elif name == "inc":
            act(A("inc%d" % r, lo, hi), A(more[0], lo, hi), ACT.Relu, scale=64.0)
        elif name == "incs":
            mm(A(more[0], lo, hi), row("ch"), A("ones", 0, n, parts=1), True, False)
            for j in range(2):
                mm(A(more[0], lo, hi), EYE, A("inc%d" % j, lo, hi), False, False)
        elif name == "gap":
            mm(A(more[0], lo, hi), A("fm", 0, 128), A(mb, lo, hi), False, False)
            whole(more[0], lo, hi, True)
        elif name == "out":
            tt(A("gout", lo, hi), A(more[0], lo, hi), A("gpi", lo, hi), ALU.add)
            store(T.yg[:, lo:hi], A("gout", lo, hi))
        else:
            raise ValueError(name)

    load("y", mine(0, 0, V), T.c0[:], "ldc")
    load("s", full("cpi"), T.cp[:], "ldp")
    load("y", full("gpi"), T.gp[:], "ldg")
    load("s", A("rfi", 0, 32), T.rf[:], "ldr")
    iota(A("J", 0, 144), [[1, 144]], 0, -1)
    iota(KS, [[16, 8], [0, 16]], 0, -1)
    iota(full("pos"), [[1, V]], -256, 0)
    for r in range(3):
        for s in ROUNDS[r].split(";"):
            w = s.split()
            if not w or (":" in w[0] and w[0][0] != str(r)):
                continue
            w[0] = w[0].split(":")[-1]
            named = len(w) > 1 and w[1] in PART
            lo, hi = PART[w[1] if named else "all"]
            run_step(r + w[0].count("+") - w[0].count("-"), w[0].strip("+-"), lo, hi, w[1 + named:])

    wait("g", "sent", total["sent"], {})
    for sem in ("qv", "qs", "qp", "qg", "st"):
        wait("y", sem, total[sem], {})
